import numpy as np
import ml_dtypes


def mxq(x, axis, fmt="e4m3"):
    dtype, down = {"e4m3": (ml_dtypes.float8_e4m3fn, 7), "e5m2": (ml_dtypes.float8_e5m2, 14)}[fmt]
    v = np.moveaxis(np.asarray(x, np.float32).astype(ml_dtypes.bfloat16).astype(np.float64), axis, -1)
    blocks = v.reshape(v.shape[:-1] + (-1, 32))
    amax = np.abs(blocks).max(-1, keepdims=True)
    byte = np.maximum(np.where(amax > 0, np.frexp(amax)[1] - 1 + 127, 0) - down, 1)
    scale = np.exp2(byte - 127.0)
    codes = (blocks / scale).astype(np.float32).astype(dtype).astype(np.float64)
    return np.moveaxis((codes * scale).reshape(v.shape), -1, axis)


WIDE = False


def mx_kscale(k):
    if not WIDE:
        return np.ones(k)
    levels = np.array([10, -10, 5, -5, 0])
    if k % 512:
        return np.exp2(np.random.permutation(np.resize(levels, k // 32))).repeat(32)
    a = np.empty((k // 512, 16))
    for p in range(k // 512):
        a[p, :8] = np.random.permutation(np.resize(levels, 8))
        for g in range(8):
            far = levels[np.abs(levels - a[p, g]) >= 10]
            a[p, g + 8] = far[np.random.randint(len(far))]
    return np.exp2(a.ravel()).repeat(32)


def f64(x):
    return np.asarray(x).astype(np.float64)


def striped(idx):
    return np.tile(idx.reshape(-1, 16).T, (8, 1)).astype(np.uint16)


def unstriped(offs):
    return offs[:16].T.reshape(-1).astype(np.int64)


def pack_weight(w):
    k, n = w.shape
    w = f64(np.asarray(w, np.float32).astype(ml_dtypes.bfloat16)).reshape(k // 32, 32, n)
    amax = np.abs(w).max(1)
    byte = np.clip(np.where(amax > 0, np.frexp(amax)[1] - 1 + 127 - 7, 1), 1, 254)
    scaled = (w * np.exp2(127.0 - byte)[:, None, :]).reshape(k, n).astype(np.float32)
    words = np.ascontiguousarray(scaled.reshape(k // 512, 128, 4, n).transpose(0, 1, 3, 2)).astype(ml_dtypes.float8_e4m3fn).view(np.uint8)
    return words, np.ascontiguousarray(byte.astype(np.uint8).reshape(k // 512, 16, n))


def unpack_weight(words, scales):
    g, p, n, _ = words.shape
    vals = np.ascontiguousarray(words).view(ml_dtypes.float8_e4m3fn).astype(np.float64) * np.repeat(np.exp2(scales.astype(np.float64) - 127.0), 8, axis=1)[..., None]
    return vals.transpose(0, 1, 3, 2).reshape(g * 512, n)


K, T, S, D, V, N = 1024, 2048, 512, 2, 256, 128
P = 2 ** 7


def setup_inputs():
    n = np.random.standard_normal
    s = mx_kscale(K)[:, None]
    packed_w1 = pack_weight(n((K, N)) / np.sqrt(K) / s)
    return {
        "xT": (n((K, T)) * s).astype(np.float32),
        "w1_words": packed_w1[0],
        "w1_scales": packed_w1[1],
        "gate": (np.tile(np.random.uniform(0.2, 1.0, (D, 1, V)) / np.sqrt(D), (1, P, 1))).astype(np.float32),
        "offs": striped(np.random.permutation(T)[:S]),
        "cen": striped(np.random.permutation(S)[:V]),
        "pos1": striped(np.random.permutation(S)[:V]),
        "pos2": striped(np.random.permutation(S)[:V]),
    }


def reference(xT, w1_words, w1_scales, gate, offs, cen, pos1, pos2):
    xq = mxq(f64(xT)[:, unstriped(offs)], 0, "e4m3")
    y = unpack_weight(w1_words, w1_scales).T @ xq
    yc = y[:, unstriped(cen)]
    return yc + (y[:, unstriped(pos1)] - yc) * f64(gate)[0, :1] + (y[:, unstriped(pos2)] - yc) * f64(gate)[1, :1]

@@ -1,0 +1,127 @@
+from contextlib import ExitStack
+
+import concourse.mybir as mybir
+
+K, T, S, V, M = 1024, 2048, 512, 256, 128
+FLOPS = 2 * K * M * S
+
+F32 = mybir.dt.float32
+BF16 = mybir.dt.bfloat16
+I32 = mybir.dt.int32
+U32 = mybir.dt.uint32
+U16 = mybir.dt.uint16
+U8 = mybir.dt.uint8
+FP8X4 = mybir.dt.float8_e4m3fn_x4
+ALU = mybir.AluOpType
+
+P = 128
+PACK = 4
+PASSES = K // (P * PACK)
+HALF = S // 2
+GROUPS = [(0, 256), (256, 128), (384, 128)]
+
+
+def tile_picked_grand_none_e_kernel(tc, xT, w1_words, w1_scales, gate, offs, cen, pos1, pos2, out):
+    nc = tc.nc
+    with ExitStack() as ctx:
+        keep = ctx.enter_context(tc.tile_pool(name="keep", bufs=1))
+        psum = ctx.enter_context(tc.psum_pool(name="psum", bufs=1))
+
+        x_rows = xT.rearrange("(z p j) t -> z j p t", p=P, j=PACK)
+        planes = [[keep.tile([P, T], F32, name="plane_%d_%d" % (z, j)) for j in range(PACK)] for z in range(PASSES)]
+        offs_sb = keep.tile([P, S // 16], U16, name="offs_sb")
+        cen_sb = keep.tile([P, V // 16], U16, name="cen_sb")
+        pos1_sb = keep.tile([P, V // 16], U16, name="pos1_sb")
+        pos2_sb = keep.tile([P, V // 16], U16, name="pos2_sb")
+        w_codes = keep.tile([P, PASSES, M], U32, name="w_codes", align_bytes=64)
+        w_scale = keep.tile([P, PASSES, M], U8, name="w_scale", align_bytes=64)
+        gates = keep.tile([P, 2, V], F32, name="gates")
+
+        nc.gpsimd.memset(w_scale[:], 0)
+        for q in range(4):
+            nc.gpsimd.dma_start(
+                out=w_scale[32 * q : 32 * q + 4, :, :].bitcast(I32),
+                in_=w1_scales[:, 4 * q : 4 * q + 4, :].rearrange("z r c -> r z c").bitcast(I32),
+            )
+
+        for z in range(PASSES):
+            for j in range(PACK):
+                nc.sync.dma_start(out=planes[z][j][:], in_=x_rows[z, j])
+                if (z, j) == (0, 0):
+                    nc.sync.dma_start(offs_sb[:], offs)
+        nc.sync.dma_start(
+            out=w_codes[:].bitcast(I32),
+            in_=w1_words.rearrange("z p c r -> p z (c r)").bitcast(I32),
+        )
+        nc.sync.dma_start(out=gates[:], in_=gate.rearrange("d p v -> p d v"))
+        nc.sync.dma_start(pos1_sb[:], pos1)
+        nc.sync.dma_start(pos2_sb[:], pos2)
+        nc.sync.dma_start(cen_sb[:], cen)
+
+        woven0 = keep.tile([P, S, PACK], BF16, name="woven0", align_bytes=64)
+        for j in range(PACK):
+            nc.vector.tensor_copy(woven0[:, :, j], planes[0][j][:].indirect(offs_sb[:]))
+        codes0 = keep.tile([P, S], U32, name="codes0", align_bytes=64)
+        scale0 = keep.tile([P, S], U8, name="scale0", align_bytes=64)
+        nc.vector.quantize_mx(out=codes0[:].bitcast(FP8X4), scales=scale0[:], in_=woven0[:].rearrange("p s j -> p (s j)"))
+
+        banks = [psum.tile([M, n], F32, name="bank_%d" % c0) for c0, n in GROUPS]
+        for bank, (c0, n) in zip(banks, GROUPS):
+            nc.tensor.matmul_mx(
+                out=bank[:],
+                lhsT=w_codes[:, 0, :].bitcast(FP8X4),
+                lhsT_scale=w_scale[:, 0, :],
+                rhs=codes0[:, c0 : c0 + n].bitcast(FP8X4),
+                rhs_scale=scale0[:, c0 : c0 + n],
+                start=True,
+                stop=False,
+            )
+
+        woven1 = [keep.tile([P, HALF, PACK], BF16, name="woven1_%d" % h, tag="woven1_%d" % h, align_bytes=64) for h in range(2)]
+        for j in range(PACK):
+            for h in range(2):
+                nc.vector.tensor_copy(
+                    woven1[h][:, :, j],
+                    planes[1][j][:].indirect(offs_sb[:, h * HALF // 16 : (h + 1) * HALF // 16]),
+                )
+        y = keep.tile([M, S], F32, name="y")
+        for g, (bank, (c0, n)) in enumerate(zip(banks, GROUPS)):
+            h, lo = divmod(c0, HALF)
+            codes1 = keep.tile([P, n], U32, name="codes1_%d" % g, align_bytes=64)
+            scale1 = keep.tile([P, n], U8, name="scale1_%d" % g, align_bytes=64)
+            nc.vector.quantize_mx(
+                out=codes1[:].bitcast(FP8X4),
+                scales=scale1[:],
+                in_=woven1[h][:, lo : lo + n, :].rearrange("p s j -> p (s j)"),
+            )
+            nc.tensor.matmul_mx(
+                out=bank[:],
+                lhsT=w_codes[:, 1, :].bitcast(FP8X4),
+                lhsT_scale=w_scale[:, 1, :],
+                rhs=codes1[:].bitcast(FP8X4),
+                rhs_scale=scale1[:],
+                start=False,
+                stop=True,
+            )
+        centre_w = keep.tile([P, V], F32, name="centre_w", tag="woven1_1", align_bytes=64)
+        nc.vector.scalar_tensor_tensor(centre_w[:], gates[:, 0, :], 1.0, gates[:, 1, :], ALU.subtract, ALU.add)
+        for g, (bank, (c0, n)) in enumerate(zip(banks, GROUPS)):
+            if g == 1:
+                nc.vector.tensor_copy(y[:, c0 : c0 + n], bank[:])
+            else:
+                nc.scalar.copy(y[:, c0 : c0 + n], bank[:])
+
+        t1 = keep.tile([M, V], F32, name="t1")
+        t2 = keep.tile([M, V], F32, name="t2")
+        t0 = keep.tile([M, V], F32, name="t0")
+        nc.vector.tensor_tensor(t1[:], y[:].indirect(pos1_sb[:]), gates[:, 0, :], ALU.mult)
+        nc.vector.tensor_tensor(t2[:], y[:].indirect(pos2_sb[:]), gates[:, 1, :], ALU.mult)
+        nc.vector.tensor_tensor(t0[:], y[:].indirect(cen_sb[:]), centre_w[:], ALU.mult)
+        halves = [slice(0, V // 2), slice(V // 2, V)]
+        pull = [keep.tile([M, V // 2], F32, name="pull_%d" % h) for h in range(2)]
+        res = [keep.tile([M, V // 2], F32, name="res_%d" % h) for h in range(2)]
+        for h in range(2):
+            nc.vector.tensor_tensor(pull[h][:], t1[:, halves[h]], t2[:, halves[h]], ALU.add)
+        for h, queue in enumerate([nc.scalar, nc.sync]):
+            nc.vector.tensor_tensor(res[h][:], pull[h][:], t0[:, halves[h]], ALU.subtract)
+            queue.dma_start(out=out[:, halves[h]], in_=res[h][:])

@@ -18,6 +18,8 @@ P = 128
 PACK = 4
 PASSES = K // (P * PACK)
 HALF = S // 2
+ORDER = [2, 0, 1]
+CHUNKS = [(0, 896), (896, 1664), (1664, 2048)]
 GROUPS = [(0, 256), (256, 128), (384, 128)]
 
 
@@ -28,7 +30,9 @@ def tile_picked_grand_none_e_kernel(tc, xT, w1_words, w1_scales, gate, offs, cen
         psum = ctx.enter_context(tc.psum_pool(name="psum", bufs=1))
 
         x_rows = xT.rearrange("(z p j) t -> z j p t", p=P, j=PACK)
-        planes = [[keep.tile([P, T], F32, name="plane_%d_%d" % (z, j)) for j in range(PACK)] for z in range(PASSES)]
+        x_pairs = xT.rearrange("(z p u e) t -> z u p e t", p=P, u=2, e=2)
+        pairs = [keep.tile([P, 2, T], F32, name="pair_%d" % u) for u in range(2)]
+        planes = [keep.tile([P, T], F32, name="plane_%d" % j, tag="plane_%d" % j, align_bytes=64) for j in range(PACK)]
         offs_sb = keep.tile([P, S // 16], U16, name="offs_sb")
         cen_sb = keep.tile([P, V // 16], U16, name="cen_sb")
         pos1_sb = keep.tile([P, V // 16], U16, name="pos1_sb")
@@ -37,18 +41,21 @@ def tile_picked_grand_none_e_kernel(tc, xT, w1_words, w1_scales, gate, offs, cen
         w_scale = keep.tile([P, PASSES, M], U8, name="w_scale", align_bytes=64)
         gates = keep.tile([P, 2, V], F32, name="gates")
 
-        nc.gpsimd.memset(w_scale[:], 0)
+        nc.vector.memset(w_scale[:].bitcast(I32), 0)
         for q in range(4):
-            nc.gpsimd.dma_start(
+            nc.scalar.dma_start(
                 out=w_scale[32 * q : 32 * q + 4, :, :].bitcast(I32),
                 in_=w1_scales[:, 4 * q : 4 * q + 4, :].rearrange("z r c -> r z c").bitcast(I32),
             )
 
-        for z in range(PASSES):
-            for j in range(PACK):
-                nc.sync.dma_start(out=planes[z][j][:], in_=x_rows[z, j])
-                if (z, j) == (0, 0):
-                    nc.sync.dma_start(offs_sb[:], offs)
+        nc.sync.dma_start(out=pairs[0][:], in_=x_pairs[0, 0])
+        nc.sync.dma_start(offs_sb[:], offs)
+        nc.sync.dma_start(out=pairs[1][:], in_=x_pairs[0, 1])
+        for j in ORDER:
+            nc.sync.dma_start(out=planes[j][:], in_=x_rows[1, j])
+        last = planes[3]
+        for a, b in CHUNKS:
+            nc.sync.dma_start(out=last[:, a:b], in_=x_rows[1, 3][:, a:b])
         nc.sync.dma_start(
             out=w_codes[:].bitcast(I32),
             in_=w1_words.rearrange("z p c r -> p z (c r)").bitcast(I32),
@@ -59,9 +66,19 @@ def tile_picked_grand_none_e_kernel(tc, xT, w1_words, w1_scales, gate, offs, cen
         nc.sync.dma_start(cen_sb[:], cen)
 
         woven0 = keep.tile([P, S, PACK], BF16, name="woven0", align_bytes=64)
-        for j in range(PACK):
-            nc.vector.tensor_copy(woven0[:, :, j], planes[0][j][:].indirect(offs_sb[:]))
-        codes0 = keep.tile([P, S], U32, name="codes0", align_bytes=64)
+        for u in range(2):
+            picked = keep.tile([P, 2, S], F32, name="picked_%d" % u)
+            for e in range(2):
+                nc.vector.tensor_copy(picked[:, e, :], pairs[u][:, e, :].indirect(offs_sb[:]))
+            nc.scalar.copy(woven0[:, :, 2 * u : 2 * u + 2], picked[:].rearrange("p e s -> p s e"))
+        woven1 = [keep.tile([P, HALF, PACK], BF16, name="woven1_%d" % h, tag="woven1_%d" % h, align_bytes=64) for h in range(2)]
+        offs_half = [offs_sb[:, h * HALF // 16 : (h + 1) * HALF // 16] for h in range(2)]
+        def gather_plane(j):
+            for h in range(2):
+                nc.vector.tensor_copy(woven1[h][:, :, j], planes[j][:].indirect(offs_half[h]))
+
+        gather_plane(ORDER[0])
+        codes0 = keep.tile([P, S], U32, name="codes0", tag="plane_%d" % ORDER[0], align_bytes=64)
         scale0 = keep.tile([P, S], U8, name="scale0", align_bytes=64)
         nc.vector.quantize_mx(out=codes0[:].bitcast(FP8X4), scales=scale0[:], in_=woven0[:].rearrange("p s j -> p (s j)"))
 
@@ -77,14 +94,17 @@ def tile_picked_grand_none_e_kernel(tc, xT, w1_words, w1_scales, gate, offs, cen
                 stop=False,
             )
 
-        woven1 = [keep.tile([P, HALF, PACK], BF16, name="woven1_%d" % h, tag="woven1_%d" % h, align_bytes=64) for h in range(2)]
-        for j in range(PACK):
-            for h in range(2):
-                nc.vector.tensor_copy(
-                    woven1[h][:, :, j],
-                    planes[1][j][:].indirect(offs_sb[:, h * HALF // 16 : (h + 1) * HALF // 16]),
-                )
-        y = keep.tile([M, S], F32, name="y")
+        for j in ORDER[1:]:
+            gather_plane(j)
+        last_bf = keep.tile([P, T], BF16, name="last_bf", tag="last_bf")
+        for i, (a, b) in enumerate(CHUNKS):
+            if i == 1:
+                nc.vector.tensor_copy(last_bf[:, a:b], last[:, a:b])
+            else:
+                nc.scalar.copy(last_bf[:, a:b], last[:, a:b])
+        nc.vector.tensor_copy(woven1[0][:, :, 3], last[:].indirect(offs_half[0]))
+        nc.scalar.activation(woven1[1][:, :, 3], last_bf[:].indirect(offs_half[1]), mybir.ActivationFunctionType.Copy)
+        y = keep.tile([M, S], F32, name="y", tag="last_bf")
         for g, (bank, (c0, n)) in enumerate(zip(banks, GROUPS)):
             h, lo = divmod(c0, HALF)
             codes1 = keep.tile([P, n], U32, name="codes1_%d" % g, align_bytes=64)

@@ -19,7 +19,9 @@ PACK = 4
 PASSES = K // (P * PACK)
 HALF = S // 2
 ORDER = [2, 0, 1]
-CHUNKS = [(0, 896), (896, 1664), (1664, 2048)]
+CHUNKS = [(0, 1152), (1152, 1664), (1664, 1920), (1920, 2048)]
+SCALAR_CASTS = [(0, 960), (1920, 2048)]
+VECTOR_CASTS = [(960, 1152), (1152, 1664), (1664, 1920)]
 GROUPS = [(0, 256), (256, 128), (384, 128)]
 
 
@@ -97,11 +99,10 @@ def tile_picked_grand_none_e_kernel(tc, xT, w1_words, w1_scales, gate, offs, cen
         for j in ORDER[1:]:
             gather_plane(j)
         last_bf = keep.tile([P, T], BF16, name="last_bf", tag="last_bf")
-        for i, (a, b) in enumerate(CHUNKS):
-            if i == 1:
-                nc.vector.tensor_copy(last_bf[:, a:b], last[:, a:b])
-            else:
-                nc.scalar.copy(last_bf[:, a:b], last[:, a:b])
+        for a, b in VECTOR_CASTS:
+            nc.vector.tensor_copy(last_bf[:, a:b], last[:, a:b])
+        for a, b in SCALAR_CASTS:
+            nc.scalar.copy(last_bf[:, a:b], last[:, a:b])
         nc.vector.tensor_copy(woven1[0][:, :, 3], last[:].indirect(offs_half[0]))
         nc.scalar.activation(woven1[1][:, :, 3], last_bf[:].indirect(offs_half[1]), mybir.ActivationFunctionType.Copy)
         y = keep.tile([M, S], F32, name="y", tag="last_bf")

@@ -18,7 +18,6 @@ P = 128
 PACK = 4
 PASSES = K // (P * PACK)
 HALF = S // 2
-ORDER = [2, 0, 1]
 CHUNKS = [(0, 1152), (1152, 1664), (1664, 1920), (1920, 2048)]
 SCALAR_CASTS = [(0, 960), (1920, 2048)]
 VECTOR_CASTS = [(960, 1152), (1152, 1664), (1664, 1920)]
@@ -34,7 +33,8 @@ def tile_picked_grand_none_e_kernel(tc, xT, w1_words, w1_scales, gate, offs, cen
         x_rows = xT.rearrange("(z p j) t -> z j p t", p=P, j=PACK)
         x_pairs = xT.rearrange("(z p u e) t -> z u p e t", p=P, u=2, e=2)
         pairs = [keep.tile([P, 2, T], F32, name="pair_%d" % u) for u in range(2)]
-        planes = [keep.tile([P, T], F32, name="plane_%d" % j, tag="plane_%d" % j, align_bytes=64) for j in range(PACK)]
+        planes = [keep.tile([P, T], F32, name="plane_%d" % j, tag="plane_%d" % j, align_bytes=64) for j in range(3)]
+        last = keep.tile([P, T], F32, name="last")
         offs_sb = keep.tile([P, S // 16], U16, name="offs_sb")
         cen_sb = keep.tile([P, V // 16], U16, name="cen_sb")
         pos1_sb = keep.tile([P, V // 16], U16, name="pos1_sb")
@@ -53,9 +53,8 @@ def tile_picked_grand_none_e_kernel(tc, xT, w1_words, w1_scales, gate, offs, cen
         nc.sync.dma_start(out=pairs[0][:], in_=x_pairs[0, 0])
         nc.sync.dma_start(offs_sb[:], offs)
         nc.sync.dma_start(out=pairs[1][:], in_=x_pairs[0, 1])
-        for j in ORDER:
+        for j in range(3):
             nc.sync.dma_start(out=planes[j][:], in_=x_rows[1, j])
-        last = planes[3]
         for a, b in CHUNKS:
             nc.sync.dma_start(out=last[:, a:b], in_=x_rows[1, 3][:, a:b])
         nc.sync.dma_start(
@@ -75,12 +74,10 @@ def tile_picked_grand_none_e_kernel(tc, xT, w1_words, w1_scales, gate, offs, cen
             nc.scalar.copy(woven0[:, :, 2 * u : 2 * u + 2], picked[:].rearrange("p e s -> p s e"))
         woven1 = [keep.tile([P, HALF, PACK], BF16, name="woven1_%d" % h, tag="woven1_%d" % h, align_bytes=64) for h in range(2)]
         offs_half = [offs_sb[:, h * HALF // 16 : (h + 1) * HALF // 16] for h in range(2)]
-        def gather_plane(j):
-            for h in range(2):
-                nc.vector.tensor_copy(woven1[h][:, :, j], planes[j][:].indirect(offs_half[h]))
-
-        gather_plane(ORDER[0])
-        codes0 = keep.tile([P, S], U32, name="codes0", tag="plane_%d" % ORDER[0], align_bytes=64)
+        picked1 = [keep.tile([P, 2, HALF], F32, name="picked1_%d" % h) for h in range(2)]
+        for h in range(2):
+            nc.vector.tensor_copy(picked1[h][:, 0, :], planes[0][:].indirect(offs_half[h]))
+        codes0 = keep.tile([P, S], U32, name="codes0", tag="plane_0", align_bytes=64)
         scale0 = keep.tile([P, S], U8, name="scale0", align_bytes=64)
         nc.vector.quantize_mx(out=codes0[:].bitcast(FP8X4), scales=scale0[:], in_=woven0[:].rearrange("p s j -> p (s j)"))
 
@@ -96,8 +93,11 @@ def tile_picked_grand_none_e_kernel(tc, xT, w1_words, w1_scales, gate, offs, cen
                 stop=False,
             )
 
-        for j in ORDER[1:]:
-            gather_plane(j)
+        for h in range(2):
+            nc.vector.tensor_copy(picked1[h][:, 1, :], planes[1][:].indirect(offs_half[h]))
+            nc.scalar.copy(woven1[h][:, :, 0:2], picked1[h][:].rearrange("p e s -> p s e"))
+        for h in range(2):
+            nc.vector.tensor_copy(woven1[h][:, :, 2], planes[2][:].indirect(offs_half[h]))
         last_bf = keep.tile([P, T], BF16, name="last_bf", tag="last_bf")
         for a, b in VECTOR_CASTS:
             nc.vector.tensor_copy(last_bf[:, a:b], last[:, a:b])

@@ -19,8 +19,8 @@ PACK = 4
 PASSES = K // (P * PACK)
 HALF = S // 2
 CHUNKS = [(0, 1152), (1152, 1664), (1664, 1920), (1920, 2048)]
-SCALAR_CASTS = [(0, 960), (1920, 2048)]
-VECTOR_CASTS = [(960, 1152), (1152, 1664), (1664, 1920)]
+SCALAR_CASTS = [(0, 512), (1920, 2048)]
+VECTOR_CASTS = [(512, 1152), (1152, 1664), (1664, 1920)]
 GROUPS = [(0, 256), (256, 128), (384, 128)]
 
 
@@ -74,7 +74,7 @@ def tile_picked_grand_none_e_kernel(tc, xT, w1_words, w1_scales, gate, offs, cen
             nc.scalar.copy(woven0[:, :, 2 * u : 2 * u + 2], picked[:].rearrange("p e s -> p s e"))
         woven1 = [keep.tile([P, HALF, PACK], BF16, name="woven1_%d" % h, tag="woven1_%d" % h, align_bytes=64) for h in range(2)]
         offs_half = [offs_sb[:, h * HALF // 16 : (h + 1) * HALF // 16] for h in range(2)]
-        picked1 = [keep.tile([P, 2, HALF], F32, name="picked1_%d" % h) for h in range(2)]
+        picked1 = [keep.tile([P, 2 + h, HALF], F32, name="picked1_%d" % h) for h in range(2)]
         for h in range(2):
             nc.vector.tensor_copy(picked1[h][:, 0, :], planes[0][:].indirect(offs_half[h]))
         codes0 = keep.tile([P, S], U32, name="codes0", tag="plane_0", align_bytes=64)
@@ -95,9 +95,10 @@ def tile_picked_grand_none_e_kernel(tc, xT, w1_words, w1_scales, gate, offs, cen
 
         for h in range(2):
             nc.vector.tensor_copy(picked1[h][:, 1, :], planes[1][:].indirect(offs_half[h]))
-            nc.scalar.copy(woven1[h][:, :, 0:2], picked1[h][:].rearrange("p e s -> p s e"))
-        for h in range(2):
-            nc.vector.tensor_copy(woven1[h][:, :, 2], planes[2][:].indirect(offs_half[h]))
+        nc.scalar.copy(woven1[0][:, :, 0:2], picked1[0][:].rearrange("p e s -> p s e"))
+        nc.vector.tensor_copy(picked1[1][:, 2, :], planes[2][:].indirect(offs_half[1]))
+        nc.scalar.copy(woven1[1][:, :, 0:3], picked1[1][:].rearrange("p e s -> p s e"))
+        nc.vector.tensor_copy(woven1[0][:, :, 2], planes[2][:].indirect(offs_half[0]))
         last_bf = keep.tile([P, T], BF16, name="last_bf", tag="last_bf")
         for a, b in VECTOR_CASTS:
             nc.vector.tensor_copy(last_bf[:, a:b], last[:, a:b])

@@ -21,7 +21,7 @@ HALF = S // 2
 CHUNKS = [(0, 1152), (1152, 1664), (1664, 1920), (1920, 2048)]
 SCALAR_CASTS = [(0, 512), (1920, 2048)]
 VECTOR_CASTS = [(512, 1152), (1152, 1664), (1664, 1920)]
-GROUPS = [(0, 256), (256, 128), (384, 128)]
+GROUPS = [(0, 128), (128, 128), (256, 128), (384, 128)]
 
 
 def tile_picked_grand_none_e_kernel(tc, xT, w1_words, w1_scales, gate, offs, cen, pos1, pos2, out):
@@ -127,11 +127,8 @@ def tile_picked_grand_none_e_kernel(tc, xT, w1_words, w1_scales, gate, offs, cen
             )
         centre_w = keep.tile([P, V], F32, name="centre_w", tag="woven1_1", align_bytes=64)
         nc.vector.scalar_tensor_tensor(centre_w[:], gates[:, 0, :], 1.0, gates[:, 1, :], ALU.subtract, ALU.add)
-        for g, (bank, (c0, n)) in enumerate(zip(banks, GROUPS)):
-            if g == 1:
-                nc.vector.tensor_copy(y[:, c0 : c0 + n], bank[:])
-            else:
-                nc.scalar.copy(y[:, c0 : c0 + n], bank[:])
+        for bank, (c0, n) in zip(banks, GROUPS):
+            nc.scalar.copy(y[:, c0 : c0 + n], bank[:])
 
         t1 = keep.tile([M, V], F32, name="t1")
         t2 = keep.tile([M, V], F32, name="t2")

@@ -132,15 +132,16 @@ def tile_picked_grand_none_e_kernel(tc, xT, w1_words, w1_scales, gate, offs, cen
 
         t1 = keep.tile([M, V], F32, name="t1")
         t2 = keep.tile([M, V], F32, name="t2")
-        t0 = keep.tile([M, V], F32, name="t0")
         nc.vector.tensor_tensor(t1[:], y[:].indirect(pos1_sb[:]), gates[:, 0, :], ALU.mult)
         nc.vector.tensor_tensor(t2[:], y[:].indirect(pos2_sb[:]), gates[:, 1, :], ALU.mult)
-        nc.vector.tensor_tensor(t0[:], y[:].indirect(cen_sb[:]), centre_w[:], ALU.mult)
         halves = [slice(0, V // 2), slice(V // 2, V)]
-        pull = [keep.tile([M, V // 2], F32, name="pull_%d" % h) for h in range(2)]
+        cen_half = [cen_sb[:, h * V // 32 : (h + 1) * V // 32] for h in range(2)]
+        t0 = [keep.tile([M, V // 2], F32, name="t0_%d" % h) for h in range(2)]
+        pull = keep.tile([M, V], F32, name="pull")
         res = [keep.tile([M, V // 2], F32, name="res_%d" % h) for h in range(2)]
-        for h in range(2):
-            nc.vector.tensor_tensor(pull[h][:], t1[:, halves[h]], t2[:, halves[h]], ALU.add)
+        nc.vector.tensor_tensor(t0[0][:], y[:].indirect(cen_half[0]), centre_w[:, halves[0]], ALU.mult)
+        nc.vector.tensor_tensor(pull[:], t1[:], t2[:], ALU.add)
+        nc.vector.tensor_tensor(t0[1][:], y[:].indirect(cen_half[1]), centre_w[:, halves[1]], ALU.mult)
         for h, queue in enumerate([nc.scalar, nc.sync]):
-            nc.vector.tensor_tensor(res[h][:], pull[h][:], t0[:, halves[h]], ALU.subtract)
+            nc.vector.tensor_tensor(res[h][:], pull[:, halves[h]], t0[h][:], ALU.subtract)
             queue.dma_start(out=out[:, halves[h]], in_=res[h][:])

@@ -19,8 +19,8 @@ PACK = 4
 PASSES = K // (P * PACK)
 HALF = S // 2
 CHUNKS = [(0, 1152), (1152, 1664), (1664, 1920), (1920, 2048)]
-SCALAR_CASTS = [(0, 512), (1920, 2048)]
-VECTOR_CASTS = [(512, 1152), (1152, 1664), (1664, 1920)]
+SCALAR_CASTS = [(0, 384), (1920, 2048)]
+VECTOR_CASTS = [(384, 1152), (1152, 1664), (1664, 1920)]
 GROUPS = [(0, 128), (128, 128), (256, 128), (384, 128)]
 
 

@@ -44,15 +44,15 @@ def tile_picked_grand_none_e_kernel(tc, xT, w1_words, w1_scales, gate, offs, cen
         gates = keep.tile([P, 2, V], F32, name="gates")
 
         nc.vector.memset(w_scale[:].bitcast(I32), 0)
-        for q in range(4):
-            nc.scalar.dma_start(
-                out=w_scale[32 * q : 32 * q + 4, :, :].bitcast(I32),
-                in_=w1_scales[:, 4 * q : 4 * q + 4, :].rearrange("z r c -> r z c").bitcast(I32),
-            )
 
         nc.sync.dma_start(out=pairs[0][:], in_=x_pairs[0, 0])
         nc.sync.dma_start(offs_sb[:], offs)
         nc.sync.dma_start(out=pairs[1][:], in_=x_pairs[0, 1])
+        for q in range(4):
+            nc.sync.dma_start(
+                out=w_scale[32 * q : 32 * q + 4, :, :].bitcast(I32),
+                in_=w1_scales[:, 4 * q : 4 * q + 4, :].rearrange("z r c -> r z c").bitcast(I32),
+            )
         for j in range(3):
             nc.sync.dma_start(out=planes[j][:], in_=x_rows[1, j])
         for a, b in CHUNKS:
@@ -142,6 +142,6 @@ def tile_picked_grand_none_e_kernel(tc, xT, w1_words, w1_scales, gate, offs, cen
         nc.vector.tensor_tensor(t0[0][:], y[:].indirect(cen_half[0]), centre_w[:, halves[0]], ALU.mult)
         nc.vector.tensor_tensor(pull[:], t1[:], t2[:], ALU.add)
         nc.vector.tensor_tensor(t0[1][:], y[:].indirect(cen_half[1]), centre_w[:, halves[1]], ALU.mult)
-        for h, queue in enumerate([nc.scalar, nc.sync]):
+        for h, queue in enumerate([nc.sync, nc.sync]):
             nc.vector.tensor_tensor(res[h][:], pull[:, halves[h]], t0[h][:], ALU.subtract)
             queue.dma_start(out=out[:, halves[h]], in_=res[h][:])

@@ -45,14 +45,16 @@ def tile_picked_grand_none_e_kernel(tc, xT, w1_words, w1_scales, gate, offs, cen
 
         nc.vector.memset(w_scale[:].bitcast(I32), 0)
 
-        nc.sync.dma_start(out=pairs[0][:], in_=x_pairs[0, 0])
-        nc.sync.dma_start(offs_sb[:], offs)
-        nc.sync.dma_start(out=pairs[1][:], in_=x_pairs[0, 1])
-        for q in range(4):
+        def load_scale_rows(q):
             nc.sync.dma_start(
                 out=w_scale[32 * q : 32 * q + 4, :, :].bitcast(I32),
                 in_=w1_scales[:, 4 * q : 4 * q + 4, :].rearrange("z r c -> r z c").bitcast(I32),
             )
+
+        nc.sync.dma_start(out=pairs[0][:], in_=x_pairs[0, 0])
+        nc.sync.dma_start(offs_sb[:], offs)
+        nc.sync.dma_start(out=pairs[1][:], in_=x_pairs[0, 1])
+        load_scale_rows(0)
         for j in range(3):
             nc.sync.dma_start(out=planes[j][:], in_=x_rows[1, j])
         for a, b in CHUNKS:
@@ -61,6 +63,8 @@ def tile_picked_grand_none_e_kernel(tc, xT, w1_words, w1_scales, gate, offs, cen
             out=w_codes[:].bitcast(I32),
             in_=w1_words.rearrange("z p c r -> p z (c r)").bitcast(I32),
         )
+        for q in range(1, 4):
+            load_scale_rows(q)
         nc.sync.dma_start(out=gates[:], in_=gate.rearrange("d p v -> p d v"))
         nc.sync.dma_start(pos1_sb[:], pos1)
         nc.sync.dma_start(pos2_sb[:], pos2)

@@ -59,12 +59,11 @@ def tile_picked_grand_none_e_kernel(tc, xT, w1_words, w1_scales, gate, offs, cen
             nc.sync.dma_start(out=planes[j][:], in_=x_rows[1, j])
         for a, b in CHUNKS:
             nc.sync.dma_start(out=last[:, a:b], in_=x_rows[1, 3][:, a:b])
-        nc.sync.dma_start(
-            out=w_codes[:].bitcast(I32),
-            in_=w1_words.rearrange("z p c r -> p z (c r)").bitcast(I32),
-        )
+        w_rows = w1_words.rearrange("z p c r -> z p (c r)")
+        nc.sync.dma_start(out=w_codes[:, 0, :].bitcast(I32), in_=w_rows[0].bitcast(I32))
         for q in range(1, 4):
             load_scale_rows(q)
+        nc.sync.dma_start(out=w_codes[:, 1, :].bitcast(I32), in_=w_rows[1].bitcast(I32))
         nc.sync.dma_start(out=gates[:], in_=gate.rearrange("d p v -> p d v"))
         nc.sync.dma_start(pos1_sb[:], pos1)
         nc.sync.dma_start(pos2_sb[:], pos2)

@@ -18,6 +18,7 @@ P = 128
 PACK = 4
 PASSES = K // (P * PACK)
 HALF = S // 2
+DMA_ALIGN = 256
 CHUNKS = [(0, 1152), (1152, 1664), (1664, 1920), (1920, 2048)]
 SCALAR_CASTS = [(0, 384), (1920, 2048)]
 VECTOR_CASTS = [(384, 1152), (1152, 1664), (1664, 1920)]
@@ -32,16 +33,16 @@ def tile_picked_grand_none_e_kernel(tc, xT, w1_words, w1_scales, gate, offs, cen
 
         x_rows = xT.rearrange("(z p j) t -> z j p t", p=P, j=PACK)
         x_pairs = xT.rearrange("(z p u e) t -> z u p e t", p=P, u=2, e=2)
-        pairs = [keep.tile([P, 2, T], F32, name="pair_%d" % u) for u in range(2)]
-        planes = [keep.tile([P, T], F32, name="plane_%d" % j, tag="plane_%d" % j, align_bytes=64) for j in range(3)]
-        last = keep.tile([P, T], F32, name="last")
+        pairs = [keep.tile([P, 2, T], F32, name="pair_%d" % u, align_bytes=DMA_ALIGN) for u in range(2)]
+        planes = [keep.tile([P, T], F32, name="plane_%d" % j, tag="plane_%d" % j, align_bytes=DMA_ALIGN) for j in range(3)]
+        last = keep.tile([P, T], F32, name="last", align_bytes=DMA_ALIGN)
         offs_sb = keep.tile([P, S // 16], U16, name="offs_sb")
         cen_sb = keep.tile([P, V // 16], U16, name="cen_sb")
         pos1_sb = keep.tile([P, V // 16], U16, name="pos1_sb")
         pos2_sb = keep.tile([P, V // 16], U16, name="pos2_sb")
-        w_codes = keep.tile([P, PASSES, M], U32, name="w_codes", align_bytes=64)
-        w_scale = keep.tile([P, PASSES, M], U8, name="w_scale", align_bytes=64)
-        gates = keep.tile([P, 2, V], F32, name="gates")
+        w_codes = keep.tile([P, PASSES, M], U32, name="w_codes", align_bytes=DMA_ALIGN)
+        w_scale = keep.tile([P, PASSES, M], U8, name="w_scale", align_bytes=DMA_ALIGN)
+        gates = keep.tile([P, 2, V], F32, name="gates", align_bytes=DMA_ALIGN)
 
         nc.vector.memset(w_scale[:].bitcast(I32), 0)
 
@@ -80,7 +81,7 @@ def tile_picked_grand_none_e_kernel(tc, xT, w1_words, w1_scales, gate, offs, cen
         picked1 = [keep.tile([P, 2 + h, HALF], F32, name="picked1_%d" % h) for h in range(2)]
         for h in range(2):
             nc.vector.tensor_copy(picked1[h][:, 0, :], planes[0][:].indirect(offs_half[h]))
-        codes0 = keep.tile([P, S], U32, name="codes0", tag="plane_0", align_bytes=64)
+        codes0 = keep.tile([P, S], U32, name="codes0", tag="plane_0", align_bytes=DMA_ALIGN)
         scale0 = keep.tile([P, S], U8, name="scale0", align_bytes=64)
         nc.vector.quantize_mx(out=codes0[:].bitcast(FP8X4), scales=scale0[:], in_=woven0[:].rearrange("p s j -> p (s j)"))
 
@@ -141,7 +142,7 @@ def tile_picked_grand_none_e_kernel(tc, xT, w1_words, w1_scales, gate, offs, cen
         cen_half = [cen_sb[:, h * V // 32 : (h + 1) * V // 32] for h in range(2)]
         t0 = [keep.tile([M, V // 2], F32, name="t0_%d" % h) for h in range(2)]
         pull = keep.tile([M, V], F32, name="pull")
-        res = [keep.tile([M, V // 2], F32, name="res_%d" % h) for h in range(2)]
+        res = [keep.tile([M, V // 2], F32, name="res_%d" % h, align_bytes=DMA_ALIGN) for h in range(2)]
         nc.vector.tensor_tensor(t0[0][:], y[:].indirect(cen_half[0]), centre_w[:, halves[0]], ALU.mult)
         nc.vector.tensor_tensor(pull[:], t1[:], t2[:], ALU.add)
         nc.vector.tensor_tensor(t0[1][:], y[:].indirect(cen_half[1]), centre_w[:, halves[1]], ALU.mult)

@@ -19,6 +19,7 @@ PACK = 4
 PASSES = K // (P * PACK)
 HALF = S // 2
 DMA_ALIGN = 256
+ROW_ALIGN = 4096
 CHUNKS = [(0, 1152), (1152, 1664), (1664, 1920), (1920, 2048)]
 SCALAR_CASTS = [(0, 384), (1920, 2048)]
 VECTOR_CASTS = [(384, 1152), (1152, 1664), (1664, 1920)]
@@ -33,13 +34,13 @@ def tile_picked_grand_none_e_kernel(tc, xT, w1_words, w1_scales, gate, offs, cen
 
         x_rows = xT.rearrange("(z p j) t -> z j p t", p=P, j=PACK)
         x_pairs = xT.rearrange("(z p u e) t -> z u p e t", p=P, u=2, e=2)
-        pairs = [keep.tile([P, 2, T], F32, name="pair_%d" % u, align_bytes=DMA_ALIGN) for u in range(2)]
-        planes = [keep.tile([P, T], F32, name="plane_%d" % j, tag="plane_%d" % j, align_bytes=DMA_ALIGN) for j in range(3)]
-        last = keep.tile([P, T], F32, name="last", align_bytes=DMA_ALIGN)
-        offs_sb = keep.tile([P, S // 16], U16, name="offs_sb")
-        cen_sb = keep.tile([P, V // 16], U16, name="cen_sb")
-        pos1_sb = keep.tile([P, V // 16], U16, name="pos1_sb")
-        pos2_sb = keep.tile([P, V // 16], U16, name="pos2_sb")
+        pairs = [keep.tile([P, 2, T], F32, name="pair_%d" % u, align_bytes=ROW_ALIGN) for u in range(2)]
+        planes = [keep.tile([P, T], F32, name="plane_%d" % j, tag="plane_%d" % j, align_bytes=ROW_ALIGN) for j in range(3)]
+        last = keep.tile([P, T], F32, name="last", align_bytes=ROW_ALIGN)
+        offs_sb = keep.tile([P, S // 16], U16, name="offs_sb", align_bytes=DMA_ALIGN)
+        cen_sb = keep.tile([P, V // 16], U16, name="cen_sb", align_bytes=DMA_ALIGN)
+        pos1_sb = keep.tile([P, V // 16], U16, name="pos1_sb", align_bytes=DMA_ALIGN)
+        pos2_sb = keep.tile([P, V // 16], U16, name="pos2_sb", align_bytes=DMA_ALIGN)
         w_codes = keep.tile([P, PASSES, M], U32, name="w_codes", align_bytes=DMA_ALIGN)
         w_scale = keep.tile([P, PASSES, M], U8, name="w_scale", align_bytes=DMA_ALIGN)
         gates = keep.tile([P, 2, V], F32, name="gates", align_bytes=DMA_ALIGN)
@@ -81,7 +82,7 @@ def tile_picked_grand_none_e_kernel(tc, xT, w1_words, w1_scales, gate, offs, cen
         picked1 = [keep.tile([P, 2 + h, HALF], F32, name="picked1_%d" % h) for h in range(2)]
         for h in range(2):
             nc.vector.tensor_copy(picked1[h][:, 0, :], planes[0][:].indirect(offs_half[h]))
-        codes0 = keep.tile([P, S], U32, name="codes0", tag="plane_0", align_bytes=DMA_ALIGN)
+        codes0 = keep.tile([P, S], U32, name="codes0", tag="plane_0", align_bytes=ROW_ALIGN)
         scale0 = keep.tile([P, S], U8, name="scale0", align_bytes=64)
         nc.vector.quantize_mx(out=codes0[:].bitcast(FP8X4), scales=scale0[:], in_=woven0[:].rearrange("p s j -> p (s j)"))
 

@@ -103,13 +103,19 @@ def tile_picked_grand_none_e_kernel(tc, xT, w1_words, w1_scales, gate, offs, cen
         nc.scalar.copy(woven1[0][:, :, 0:2], picked1[0][:].rearrange("p e s -> p s e"))
         nc.vector.tensor_copy(picked1[1][:, 2, :], planes[2][:].indirect(offs_half[1]))
         nc.scalar.copy(woven1[1][:, :, 0:3], picked1[1][:].rearrange("p e s -> p s e"))
-        nc.vector.tensor_copy(woven1[0][:, :, 2], planes[2][:].indirect(offs_half[0]))
+        late = [keep.tile([P, 2, HALF // 2], BF16, name="late_%d" % g) for g in range(2)]
+        offs_quarter = [offs_sb[:, g * HALF // 32 : (g + 1) * HALF // 32] for g in range(2)]
+        for g in range(2):
+            nc.vector.tensor_copy(late[g][:, 0, :], planes[2][:].indirect(offs_quarter[g]))
         last_bf = keep.tile([P, T], BF16, name="last_bf", tag="last_bf")
         for a, b in VECTOR_CASTS:
             nc.vector.tensor_copy(last_bf[:, a:b], last[:, a:b])
         for a, b in SCALAR_CASTS:
             nc.scalar.copy(last_bf[:, a:b], last[:, a:b])
-        nc.vector.tensor_copy(woven1[0][:, :, 3], last[:].indirect(offs_half[0]))
+        for g in range(2):
+            nc.vector.tensor_copy(late[g][:, 1, :], last[:].indirect(offs_quarter[g]))
+        for g in range(2):
+            nc.vector.tensor_copy(woven1[0][:, g * HALF // 2 : (g + 1) * HALF // 2, 2:4], late[g][:].rearrange("p e s -> p s e"))
         nc.scalar.activation(woven1[1][:, :, 3], last_bf[:].indirect(offs_half[1]), mybir.ActivationFunctionType.Copy)
         y = keep.tile([M, S], F32, name="y", tag="last_bf")
         for g, (bank, (c0, n)) in enumerate(zip(banks, GROUPS)):

@@ -21,8 +21,8 @@ HALF = S // 2
 DMA_ALIGN = 256
 ROW_ALIGN = 4096
 CHUNKS = [(0, 1152), (1152, 1664), (1664, 1920), (1920, 2048)]
-SCALAR_CASTS = [(0, 384), (1920, 2048)]
-VECTOR_CASTS = [(384, 1152), (1152, 1664), (1664, 1920)]
+SCALAR_CASTS = [(0, 256), (1920, 2048)]
+VECTOR_CASTS = [(256, 1152), (1152, 1664), (1664, 1920)]
 GROUPS = [(0, 128), (128, 128), (256, 128), (384, 128)]
 
 

@@ -56,14 +56,15 @@ def tile_picked_grand_none_e_kernel(tc, xT, w1_words, w1_scales, gate, offs, cen
         nc.sync.dma_start(out=pairs[0][:], in_=x_pairs[0, 0])
         nc.sync.dma_start(offs_sb[:], offs)
         nc.sync.dma_start(out=pairs[1][:], in_=x_pairs[0, 1])
-        load_scale_rows(0)
+        for q in range(2):
+            load_scale_rows(q)
         for j in range(3):
             nc.sync.dma_start(out=planes[j][:], in_=x_rows[1, j])
         for a, b in CHUNKS:
             nc.sync.dma_start(out=last[:, a:b], in_=x_rows[1, 3][:, a:b])
         w_rows = w1_words.rearrange("z p c r -> z p (c r)")
         nc.sync.dma_start(out=w_codes[:, 0, :].bitcast(I32), in_=w_rows[0].bitcast(I32))
-        for q in range(1, 4):
+        for q in range(2, 4):
             load_scale_rows(q)
         nc.sync.dma_start(out=w_codes[:, 1, :].bitcast(I32), in_=w_rows[1].bitcast(I32))
         nc.sync.dma_start(out=gates[:], in_=gate.rearrange("d p v -> p d v"))
@@ -145,14 +146,21 @@ def tile_picked_grand_none_e_kernel(tc, xT, w1_words, w1_scales, gate, offs, cen
         t2 = keep.tile([M, V], F32, name="t2")
         nc.vector.tensor_tensor(t1[:], y[:].indirect(pos1_sb[:]), gates[:, 0, :], ALU.mult)
         nc.vector.tensor_tensor(t2[:], y[:].indirect(pos2_sb[:]), gates[:, 1, :], ALU.mult)
-        halves = [slice(0, V // 2), slice(V // 2, V)]
-        cen_half = [cen_sb[:, h * V // 32 : (h + 1) * V // 32] for h in range(2)]
-        t0 = [keep.tile([M, V // 2], F32, name="t0_%d" % h) for h in range(2)]
+        parts = [(0, 128), (128, 192), (192, 256)]
+        t0 = [keep.tile([M, b - a], F32, name="t0_%d" % a) for a, b in parts]
         pull = keep.tile([M, V], F32, name="pull")
         res = [keep.tile([M, V // 2], F32, name="res_%d" % h, align_bytes=DMA_ALIGN) for h in range(2)]
-        nc.vector.tensor_tensor(t0[0][:], y[:].indirect(cen_half[0]), centre_w[:, halves[0]], ALU.mult)
+
+        def centre_term(i):
+            a, b = parts[i]
+            nc.vector.tensor_tensor(t0[i][:], y[:].indirect(cen_sb[:, a // 16 : b // 16]), centre_w[:, a:b], ALU.mult)
+
+        centre_term(0)
         nc.vector.tensor_tensor(pull[:], t1[:], t2[:], ALU.add)
-        nc.vector.tensor_tensor(t0[1][:], y[:].indirect(cen_half[1]), centre_w[:, halves[1]], ALU.mult)
-        for h, queue in enumerate([nc.sync, nc.sync]):
-            nc.vector.tensor_tensor(res[h][:], pull[:, halves[h]], t0[h][:], ALU.subtract)
-            queue.dma_start(out=out[:, halves[h]], in_=res[h][:])
+        centre_term(1)
+        centre_term(2)
+        for i, (a, b) in enumerate(parts):
+            h, lo = divmod(a, V // 2)
+            nc.vector.tensor_tensor(res[h][:, lo : lo + b - a], pull[:, a:b], t0[i][:], ALU.subtract)
+            if b % (V // 2) == 0:
+                nc.sync.dma_start(out=out[:, h * V // 2 : (h + 1) * V // 2], in_=res[h][:])

@@ -21,8 +21,8 @@ HALF = S // 2
 DMA_ALIGN = 256
 ROW_ALIGN = 4096
 CHUNKS = [(0, 1152), (1152, 1664), (1664, 1920), (1920, 2048)]
-SCALAR_CASTS = [(0, 256), (1920, 2048)]
-VECTOR_CASTS = [(256, 1152), (1152, 1664), (1664, 1920)]
+SCALAR_CASTS = [(0, 256), (1792, 1920), (1920, 2048)]
+VECTOR_CASTS = [(256, 1152), (1152, 1664), (1664, 1792)]
 GROUPS = [(0, 128), (128, 128), (256, 128), (384, 128)]
 
 

@@ -80,7 +80,7 @@ def tile_picked_grand_none_e_kernel(tc, xT, w1_words, w1_scales, gate, offs, cen
             nc.scalar.copy(woven0[:, :, 2 * u : 2 * u + 2], picked[:].rearrange("p e s -> p s e"))
         woven1 = [keep.tile([P, HALF, PACK], BF16, name="woven1_%d" % h, tag="woven1_%d" % h, align_bytes=64) for h in range(2)]
         offs_half = [offs_sb[:, h * HALF // 16 : (h + 1) * HALF // 16] for h in range(2)]
-        picked1 = [keep.tile([P, 2 + h, HALF], F32, name="picked1_%d" % h) for h in range(2)]
+        picked1 = [keep.tile([P, 2 + h, HALF], BF16, name="picked1_%d" % h) for h in range(2)]
         for h in range(2):
             nc.vector.tensor_copy(picked1[h][:, 0, :], planes[0][:].indirect(offs_half[h]))
         codes0 = keep.tile([P, S], U32, name="codes0", tag="plane_0", align_bytes=ROW_ALIGN)
@@ -102,10 +102,12 @@ def tile_picked_grand_none_e_kernel(tc, xT, w1_words, w1_scales, gate, offs, cen
         for h in range(2):
             nc.vector.tensor_copy(picked1[h][:, 1, :], planes[1][:].indirect(offs_half[h]))
         nc.scalar.copy(woven1[0][:, :, 0:2], picked1[0][:].rearrange("p e s -> p s e"))
-        nc.vector.tensor_copy(picked1[1][:, 2, :], planes[2][:].indirect(offs_half[1]))
-        nc.scalar.copy(woven1[1][:, :, 0:3], picked1[1][:].rearrange("p e s -> p s e"))
+        offs_quarter = [offs_sb[:, g * HALF // 32 : (g + 1) * HALF // 32] for g in range(4)]
+        for g in range(2):
+            cols = slice(g * HALF // 2, (g + 1) * HALF // 2)
+            nc.vector.tensor_copy(picked1[1][:, 2, cols], planes[2][:].indirect(offs_quarter[2 + g]))
+            nc.scalar.copy(woven1[1][:, cols, 0:3], picked1[1][:, :, cols].rearrange("p e s -> p s e"))
         late = [keep.tile([P, 2, HALF // 2], BF16, name="late_%d" % g) for g in range(2)]
-        offs_quarter = [offs_sb[:, g * HALF // 32 : (g + 1) * HALF // 32] for g in range(2)]
         for g in range(2):
             nc.vector.tensor_copy(late[g][:, 0, :], planes[2][:].indirect(offs_quarter[g]))
         last_bf = keep.tile([P, T], BF16, name="last_bf", tag="last_bf")

@@ -13,17 +13,19 @@ U16 = mybir.dt.uint16
 U8 = mybir.dt.uint8
 FP8X4 = mybir.dt.float8_e4m3fn_x4
 ALU = mybir.AluOpType
+COPY = mybir.ActivationFunctionType.Copy
 
 P = 128
 PACK = 4
 PASSES = K // (P * PACK)
 HALF = S // 2
-DMA_ALIGN = 256
-ROW_ALIGN = 4096
-CHUNKS = [(0, 1152), (1152, 1664), (1664, 1920), (1920, 2048)]
-SCALAR_CASTS = [(0, 256), (1792, 1920), (1920, 2048)]
-VECTOR_CASTS = [(256, 1152), (1152, 1664), (1664, 1792)]
-GROUPS = [(0, 128), (128, 128), (256, 128), (384, 128)]
+GROUP = 128
+ALIGN = 256
+CHUNKS = [(0, 1408), (1408, 1920), (1920, 2048)]
+SCALAR_CASTS = [(0, 448), (1408, 1568), (1920, 2048)]
+VECTOR_CASTS = [(448, 1408), (1568, 1920)]
+PARTS = [(0, 128), (128, 192), (192, 256)]
+STORES = [(0, 128), (128, 256)]
 
 
 def tile_picked_grand_none_e_kernel(tc, xT, w1_words, w1_scales, gate, offs, cen, pos1, pos2, out):
@@ -32,18 +34,19 @@ def tile_picked_grand_none_e_kernel(tc, xT, w1_words, w1_scales, gate, offs, cen
         keep = ctx.enter_context(tc.tile_pool(name="keep", bufs=1))
         psum = ctx.enter_context(tc.psum_pool(name="psum", bufs=1))
 
-        x_rows = xT.rearrange("(z p j) t -> z j p t", p=P, j=PACK)
-        x_pairs = xT.rearrange("(z p u e) t -> z u p e t", p=P, u=2, e=2)
-        pairs = [keep.tile([P, 2, T], F32, name="pair_%d" % u, align_bytes=ROW_ALIGN) for u in range(2)]
-        planes = [keep.tile([P, T], F32, name="plane_%d" % j, tag="plane_%d" % j, align_bytes=ROW_ALIGN) for j in range(3)]
-        last = keep.tile([P, T], F32, name="last", align_bytes=ROW_ALIGN)
-        offs_sb = keep.tile([P, S // 16], U16, name="offs_sb", align_bytes=DMA_ALIGN)
-        cen_sb = keep.tile([P, V // 16], U16, name="cen_sb", align_bytes=DMA_ALIGN)
-        pos1_sb = keep.tile([P, V // 16], U16, name="pos1_sb", align_bytes=DMA_ALIGN)
-        pos2_sb = keep.tile([P, V // 16], U16, name="pos2_sb", align_bytes=DMA_ALIGN)
-        w_codes = keep.tile([P, PASSES, M], U32, name="w_codes", align_bytes=DMA_ALIGN)
-        w_scale = keep.tile([P, PASSES, M], U8, name="w_scale", align_bytes=DMA_ALIGN)
-        gates = keep.tile([P, 2, V], F32, name="gates", align_bytes=DMA_ALIGN)
+        by_pass = xT.rearrange("(z p j) t -> z p j t", p=P, j=PACK)
+        pairs = [keep.tile([P, 2, T], F32, name="pair_%d" % u, align_bytes=ALIGN) for u in range(2)]
+        plane0 = keep.tile([P, T], F32, name="plane0", tag="plane0", align_bytes=ALIGN)
+        plane1 = keep.tile([P, T], F32, name="plane1", align_bytes=ALIGN)
+        plane2 = keep.tile([P, T], F32, name="plane2", align_bytes=ALIGN)
+        plane3 = keep.tile([P, T], F32, name="plane3", align_bytes=ALIGN)
+        offs_sb = keep.tile([P, S // 16], U16, name="offs_sb", align_bytes=ALIGN)
+        cen_sb = keep.tile([P, V // 16], U16, name="cen_sb", align_bytes=ALIGN)
+        pos1_sb = keep.tile([P, V // 16], U16, name="pos1_sb", align_bytes=ALIGN)
+        pos2_sb = keep.tile([P, V // 16], U16, name="pos2_sb", align_bytes=ALIGN)
+        w_codes = keep.tile([P, PASSES, M], U32, name="w_codes", align_bytes=ALIGN)
+        w_scale = keep.tile([P, PASSES, M], U8, name="w_scale", align_bytes=ALIGN)
+        gates = keep.tile([P, 2, V], F32, name="gates", align_bytes=ALIGN)
 
         nc.vector.memset(w_scale[:].bitcast(I32), 0)
 
@@ -53,15 +56,16 @@ def tile_picked_grand_none_e_kernel(tc, xT, w1_words, w1_scales, gate, offs, cen
                 in_=w1_scales[:, 4 * q : 4 * q + 4, :].rearrange("z r c -> r z c").bitcast(I32),
             )
 
-        nc.sync.dma_start(out=pairs[0][:], in_=x_pairs[0, 0])
+        nc.sync.dma_start(out=pairs[0][:], in_=by_pass[0][:, 0:2, :])
         nc.sync.dma_start(offs_sb[:], offs)
-        nc.sync.dma_start(out=pairs[1][:], in_=x_pairs[0, 1])
+        nc.sync.dma_start(out=pairs[1][:], in_=by_pass[0][:, 2:4, :])
         for q in range(2):
             load_scale_rows(q)
-        for j in range(3):
-            nc.sync.dma_start(out=planes[j][:], in_=x_rows[1, j])
+        nc.sync.dma_start(out=plane0[:], in_=by_pass[1][:, 0, :])
+        nc.sync.dma_start(out=plane1[:], in_=by_pass[1][:, 1, :])
+        nc.sync.dma_start(out=plane2[:], in_=by_pass[1][:, 2, :])
         for a, b in CHUNKS:
-            nc.sync.dma_start(out=last[:, a:b], in_=x_rows[1, 3][:, a:b])
+            nc.sync.dma_start(out=plane3[:, a:b], in_=by_pass[1][:, 3, a:b])
         w_rows = w1_words.rearrange("z p c r -> z p (c r)")
         nc.sync.dma_start(out=w_codes[:, 0, :].bitcast(I32), in_=w_rows[0].bitcast(I32))
         for q in range(2, 4):
@@ -72,63 +76,71 @@ def tile_picked_grand_none_e_kernel(tc, xT, w1_words, w1_scales, gate, offs, cen
         nc.sync.dma_start(pos2_sb[:], pos2)
         nc.sync.dma_start(cen_sb[:], cen)
 
-        woven0 = keep.tile([P, S, PACK], BF16, name="woven0", align_bytes=64)
-        for u in range(2):
-            picked = keep.tile([P, 2, S], F32, name="picked_%d" % u)
-            for e in range(2):
-                nc.vector.tensor_copy(picked[:, e, :], pairs[u][:, e, :].indirect(offs_sb[:]))
-            nc.scalar.copy(woven0[:, :, 2 * u : 2 * u + 2], picked[:].rearrange("p e s -> p s e"))
-        woven1 = [keep.tile([P, HALF, PACK], BF16, name="woven1_%d" % h, tag="woven1_%d" % h, align_bytes=64) for h in range(2)]
         offs_half = [offs_sb[:, h * HALF // 16 : (h + 1) * HALF // 16] for h in range(2)]
-        picked1 = [keep.tile([P, 2 + h, HALF], BF16, name="picked1_%d" % h) for h in range(2)]
+        offs_group = [offs_sb[:, g * GROUP // 16 : (g + 1) * GROUP // 16] for g in range(4)]
+
+        woven0 = keep.tile([P, S, PACK], BF16, name="woven0", align_bytes=64)
+        picked0 = [keep.tile([P, 2, S], F32, name="picked0_%d" % u) for u in range(2)]
+        for e in range(2):
+            nc.vector.tensor_copy(picked0[0][:, e, :], pairs[0][:, e, :].indirect(offs_sb[:]))
+        nc.scalar.copy(woven0[:, :, 0:2], picked0[0][:].rearrange("p e s -> p s e"))
         for h in range(2):
-            nc.vector.tensor_copy(picked1[h][:, 0, :], planes[0][:].indirect(offs_half[h]))
-        codes0 = keep.tile([P, S], U32, name="codes0", tag="plane_0", align_bytes=ROW_ALIGN)
+            cols = slice(h * HALF, (h + 1) * HALF)
+            for e in range(2):
+                nc.vector.tensor_copy(picked0[1][:, e, cols], pairs[1][:, e, :].indirect(offs_half[h]))
+            nc.scalar.copy(woven0[:, cols, 2:4], picked0[1][:, :, cols].rearrange("p e s -> p s e"))
+
+        woven1 = [keep.tile([P, HALF, PACK], BF16, name="woven1_%d" % h, tag="woven1_%d" % h, align_bytes=64) for h in range(2)]
+        picked1 = [keep.tile([P, 2, HALF], BF16, name="picked1_%d" % h) for h in range(2)]
+        for h in range(2):
+            nc.vector.tensor_copy(picked1[h][:, 0, :], plane0[:].indirect(offs_half[h]))
+        codes0 = keep.tile([P, S], U32, name="codes0", tag="plane0", align_bytes=ALIGN)
         scale0 = keep.tile([P, S], U8, name="scale0", align_bytes=64)
         nc.vector.quantize_mx(out=codes0[:].bitcast(FP8X4), scales=scale0[:], in_=woven0[:].rearrange("p s j -> p (s j)"))
+        for h in (1, 0):
+            nc.vector.tensor_copy(picked1[h][:, 1, :], plane1[:].indirect(offs_half[h]))
+        nc.scalar.copy(woven1[1][:, :, 0:2], picked1[1][:].rearrange("p e s -> p s e"))
+        nc.vector.tensor_copy(woven1[0][:, :, 0:2], picked1[0][:].rearrange("p e s -> p s e"))
 
-        banks = [psum.tile([M, n], F32, name="bank_%d" % c0) for c0, n in GROUPS]
-        for bank, (c0, n) in zip(banks, GROUPS):
+        banks = [psum.tile([M, GROUP], F32, name="bank_%d" % g) for g in range(4)]
+        for g, bank in enumerate(banks):
+            cols = slice(g * GROUP, (g + 1) * GROUP)
             nc.tensor.matmul_mx(
                 out=bank[:],
                 lhsT=w_codes[:, 0, :].bitcast(FP8X4),
                 lhsT_scale=w_scale[:, 0, :],
-                rhs=codes0[:, c0 : c0 + n].bitcast(FP8X4),
-                rhs_scale=scale0[:, c0 : c0 + n],
+                rhs=codes0[:, cols].bitcast(FP8X4),
+                rhs_scale=scale0[:, cols],
                 start=True,
                 stop=False,
             )
 
-        for h in range(2):
-            nc.vector.tensor_copy(picked1[h][:, 1, :], planes[1][:].indirect(offs_half[h]))
-        nc.scalar.copy(woven1[0][:, :, 0:2], picked1[0][:].rearrange("p e s -> p s e"))
-        offs_quarter = [offs_sb[:, g * HALF // 32 : (g + 1) * HALF // 32] for g in range(4)]
         for g in range(2):
-            cols = slice(g * HALF // 2, (g + 1) * HALF // 2)
-            nc.vector.tensor_copy(picked1[1][:, 2, cols], planes[2][:].indirect(offs_quarter[2 + g]))
-            nc.scalar.copy(woven1[1][:, cols, 0:3], picked1[1][:, :, cols].rearrange("p e s -> p s e"))
-        late = [keep.tile([P, 2, HALF // 2], BF16, name="late_%d" % g) for g in range(2)]
+            third = keep.tile([P, GROUP], BF16, name="third_%d" % g)
+            nc.vector.tensor_copy(third[:], plane2[:].indirect(offs_group[2 + g]))
+            nc.scalar.copy(woven1[1][:, g * GROUP : (g + 1) * GROUP, 2], third[:])
+        late = [keep.tile([P, 2, GROUP], BF16, name="late_%d" % g) for g in range(2)]
         for g in range(2):
-            nc.vector.tensor_copy(late[g][:, 0, :], planes[2][:].indirect(offs_quarter[g]))
-        last_bf = keep.tile([P, T], BF16, name="last_bf", tag="last_bf")
+            nc.vector.tensor_copy(late[g][:, 0, :], plane2[:].indirect(offs_group[g]))
+        plane3_bf = keep.tile([P, T], BF16, name="plane3_bf", tag="plane3_bf")
         for a, b in VECTOR_CASTS:
-            nc.vector.tensor_copy(last_bf[:, a:b], last[:, a:b])
+            nc.vector.tensor_copy(plane3_bf[:, a:b], plane3[:, a:b])
         for a, b in SCALAR_CASTS:
-            nc.scalar.copy(last_bf[:, a:b], last[:, a:b])
+            nc.scalar.copy(plane3_bf[:, a:b], plane3[:, a:b])
         for g in range(2):
-            nc.vector.tensor_copy(late[g][:, 1, :], last[:].indirect(offs_quarter[g]))
+            nc.vector.tensor_copy(late[g][:, 1, :], plane3[:].indirect(offs_group[g]))
         for g in range(2):
-            nc.vector.tensor_copy(woven1[0][:, g * HALF // 2 : (g + 1) * HALF // 2, 2:4], late[g][:].rearrange("p e s -> p s e"))
-        nc.scalar.activation(woven1[1][:, :, 3], last_bf[:].indirect(offs_half[1]), mybir.ActivationFunctionType.Copy)
-        y = keep.tile([M, S], F32, name="y", tag="last_bf")
-        for g, (bank, (c0, n)) in enumerate(zip(banks, GROUPS)):
-            h, lo = divmod(c0, HALF)
-            codes1 = keep.tile([P, n], U32, name="codes1_%d" % g, align_bytes=64)
-            scale1 = keep.tile([P, n], U8, name="scale1_%d" % g, align_bytes=64)
+            nc.vector.tensor_copy(woven1[0][:, g * GROUP : (g + 1) * GROUP, 2:4], late[g][:].rearrange("p e s -> p s e"))
+        nc.scalar.activation(woven1[1][:, :, 3], plane3_bf[:].indirect(offs_half[1]), COPY)
+        y = keep.tile([M, S], F32, name="y", tag="plane3_bf")
+        for g, bank in enumerate(banks):
+            h, lo = divmod(g * GROUP, HALF)
+            codes1 = keep.tile([P, GROUP], U32, name="codes1_%d" % g, align_bytes=64)
+            scale1 = keep.tile([P, GROUP], U8, name="scale1_%d" % g, align_bytes=64)
             nc.vector.quantize_mx(
                 out=codes1[:].bitcast(FP8X4),
                 scales=scale1[:],
-                in_=woven1[h][:, lo : lo + n, :].rearrange("p s j -> p (s j)"),
+                in_=woven1[h][:, lo : lo + GROUP, :].rearrange("p s j -> p (s j)"),
             )
             nc.tensor.matmul_mx(
                 out=bank[:],
@@ -141,28 +153,26 @@ def tile_picked_grand_none_e_kernel(tc, xT, w1_words, w1_scales, gate, offs, cen
             )
         centre_w = keep.tile([P, V], F32, name="centre_w", tag="woven1_1", align_bytes=64)
         nc.vector.scalar_tensor_tensor(centre_w[:], gates[:, 0, :], 1.0, gates[:, 1, :], ALU.subtract, ALU.add)
-        for bank, (c0, n) in zip(banks, GROUPS):
-            nc.scalar.copy(y[:, c0 : c0 + n], bank[:])
+        for g, bank in enumerate(banks):
+            nc.scalar.copy(y[:, g * GROUP : (g + 1) * GROUP], bank[:])
 
         t1 = keep.tile([M, V], F32, name="t1")
         t2 = keep.tile([M, V], F32, name="t2")
         nc.vector.tensor_tensor(t1[:], y[:].indirect(pos1_sb[:]), gates[:, 0, :], ALU.mult)
         nc.vector.tensor_tensor(t2[:], y[:].indirect(pos2_sb[:]), gates[:, 1, :], ALU.mult)
-        parts = [(0, 128), (128, 192), (192, 256)]
-        t0 = [keep.tile([M, b - a], F32, name="t0_%d" % a) for a, b in parts]
+        t0 = [keep.tile([M, b - a], F32, name="t0_%d" % a) for a, b in PARTS]
         pull = keep.tile([M, V], F32, name="pull")
-        res = [keep.tile([M, V // 2], F32, name="res_%d" % h, align_bytes=DMA_ALIGN) for h in range(2)]
+        res = keep.tile([M, V], F32, name="res", align_bytes=ALIGN)
 
         def centre_term(i):
-            a, b = parts[i]
+            a, b = PARTS[i]
             nc.vector.tensor_tensor(t0[i][:], y[:].indirect(cen_sb[:, a // 16 : b // 16]), centre_w[:, a:b], ALU.mult)
 
         centre_term(0)
         nc.vector.tensor_tensor(pull[:], t1[:], t2[:], ALU.add)
         centre_term(1)
         centre_term(2)
-        for i, (a, b) in enumerate(parts):
-            h, lo = divmod(a, V // 2)
-            nc.vector.tensor_tensor(res[h][:, lo : lo + b - a], pull[:, a:b], t0[i][:], ALU.subtract)
-            if b % (V // 2) == 0:
-                nc.sync.dma_start(out=out[:, h * V // 2 : (h + 1) * V // 2], in_=res[h][:])
+        for i, (a, b) in enumerate(PARTS):
+            nc.vector.tensor_tensor(res[:, a:b], pull[:, a:b], t0[i][:], ALU.subtract)
+        for a, b in STORES:
+            nc.sync.dma_start(out=out[:, a:b], in_=res[:, a:b])

@@ -71,7 +71,8 @@ def tile_picked_grand_none_e_kernel(tc, xT, w1_words, w1_scales, gate, offs, cen
         for q in range(2, 4):
             load_scale_rows(q)
         nc.sync.dma_start(out=w_codes[:, 1, :].bitcast(I32), in_=w_rows[1].bitcast(I32))
-        nc.sync.dma_start(out=gates[:], in_=gate.rearrange("d p v -> p d v"))
+        for d in range(2):
+            nc.sync.dma_start(out=gates[:, d, :], in_=gate[d])
         nc.sync.dma_start(pos1_sb[:], pos1)
         nc.sync.dma_start(pos2_sb[:], pos2)
         nc.sync.dma_start(cen_sb[:], cen)

@@ -21,11 +21,6 @@ PASSES = K // (P * PACK)
 HALF = S // 2
 GROUP = 128
 ALIGN = 256
-CHUNKS = [(0, 1408), (1408, 1920), (1920, 2048)]
-SCALAR_CASTS = [(0, 448), (1408, 1568), (1920, 2048)]
-VECTOR_CASTS = [(448, 1408), (1568, 1920)]
-PARTS = [(0, 128), (128, 192), (192, 256)]
-STORES = [(0, 128), (128, 256)]
 
 
 def tile_picked_grand_none_e_kernel(tc, xT, w1_words, w1_scales, gate, offs, cen, pos1, pos2, out):
@@ -35,9 +30,8 @@ def tile_picked_grand_none_e_kernel(tc, xT, w1_words, w1_scales, gate, offs, cen
         psum = ctx.enter_context(tc.psum_pool(name="psum", bufs=1))
 
         by_pass = xT.rearrange("(z p j) t -> z p j t", p=P, j=PACK)
-        pairs = [keep.tile([P, 2, T], F32, name="pair_%d" % u, align_bytes=ALIGN) for u in range(2)]
-        plane0 = keep.tile([P, T], F32, name="plane0", tag="plane0", align_bytes=ALIGN)
-        plane1 = keep.tile([P, T], F32, name="plane1", align_bytes=ALIGN)
+        x0 = keep.tile([P, PACK, T], F32, name="x0", align_bytes=ALIGN)
+        x1_pair = keep.tile([P, 2, T], F32, name="x1_pair", align_bytes=ALIGN)
         plane2 = keep.tile([P, T], F32, name="plane2", align_bytes=ALIGN)
         plane3 = keep.tile([P, T], F32, name="plane3", align_bytes=ALIGN)
         offs_sb = keep.tile([P, S // 16], U16, name="offs_sb", align_bytes=ALIGN)
@@ -50,58 +44,41 @@ def tile_picked_grand_none_e_kernel(tc, xT, w1_words, w1_scales, gate, offs, cen
 
         nc.vector.memset(w_scale[:].bitcast(I32), 0)
 
-        def load_scale_rows(q):
+        warm = keep.tile([P, 2], F32, name="warm")
+        nc.vector.memset(warm[:, 0:1], 0.0)
+        nc.scalar.activation(warm[:, 1:2], warm[:, 0:1], COPY)
+
+        nc.sync.dma_start(offs_sb[:], offs)
+        nc.sync.dma_start(out=x0[:], in_=by_pass[0])
+        for q in range(4):
             nc.sync.dma_start(
                 out=w_scale[32 * q : 32 * q + 4, :, :].bitcast(I32),
                 in_=w1_scales[:, 4 * q : 4 * q + 4, :].rearrange("z r c -> r z c").bitcast(I32),
             )
-
-        nc.sync.dma_start(out=pairs[0][:], in_=by_pass[0][:, 0:2, :])
-        nc.sync.dma_start(offs_sb[:], offs)
-        nc.sync.dma_start(out=pairs[1][:], in_=by_pass[0][:, 2:4, :])
-        for q in range(2):
-            load_scale_rows(q)
-        nc.sync.dma_start(out=plane0[:], in_=by_pass[1][:, 0, :])
-        nc.sync.dma_start(out=plane1[:], in_=by_pass[1][:, 1, :])
+        nc.sync.dma_start(out=x1_pair[:], in_=by_pass[1][:, 0:2, :])
         nc.sync.dma_start(out=plane2[:], in_=by_pass[1][:, 2, :])
-        for a, b in CHUNKS:
-            nc.sync.dma_start(out=plane3[:, a:b], in_=by_pass[1][:, 3, a:b])
-        w_rows = w1_words.rearrange("z p c r -> z p (c r)")
-        nc.sync.dma_start(out=w_codes[:, 0, :].bitcast(I32), in_=w_rows[0].bitcast(I32))
-        for q in range(2, 4):
-            load_scale_rows(q)
-        nc.sync.dma_start(out=w_codes[:, 1, :].bitcast(I32), in_=w_rows[1].bitcast(I32))
-        for d in range(2):
-            nc.sync.dma_start(out=gates[:, d, :], in_=gate[d])
+        nc.sync.dma_start(out=plane3[:], in_=by_pass[1][:, 3, :])
+        nc.sync.dma_start(out=w_codes[:].bitcast(I32), in_=w1_words.rearrange("z p c r -> p z (c r)").bitcast(I32))
+        nc.sync.dma_start(out=gates[:], in_=gate.rearrange("d p v -> p d v"))
         nc.sync.dma_start(pos1_sb[:], pos1)
-        nc.sync.dma_start(pos2_sb[:], pos2)
         nc.sync.dma_start(cen_sb[:], cen)
+        nc.sync.dma_start(pos2_sb[:], pos2)
 
         offs_half = [offs_sb[:, h * HALF // 16 : (h + 1) * HALF // 16] for h in range(2)]
         offs_group = [offs_sb[:, g * GROUP // 16 : (g + 1) * GROUP // 16] for g in range(4)]
 
         woven0 = keep.tile([P, S, PACK], BF16, name="woven0", align_bytes=64)
-        picked0 = [keep.tile([P, 2, S], F32, name="picked0_%d" % u) for u in range(2)]
-        for e in range(2):
-            nc.vector.tensor_copy(picked0[0][:, e, :], pairs[0][:, e, :].indirect(offs_sb[:]))
-        nc.scalar.copy(woven0[:, :, 0:2], picked0[0][:].rearrange("p e s -> p s e"))
+        picked0 = [keep.tile([P, 2, HALF], F32, name="picked0_%d" % h) for h in range(2)]
+        for j in range(2):
+            nc.vector.tensor_copy(woven0[:, :, j], x0[:, j, :].indirect(offs_sb[:]))
         for h in range(2):
-            cols = slice(h * HALF, (h + 1) * HALF)
             for e in range(2):
-                nc.vector.tensor_copy(picked0[1][:, e, cols], pairs[1][:, e, :].indirect(offs_half[h]))
-            nc.scalar.copy(woven0[:, cols, 2:4], picked0[1][:, :, cols].rearrange("p e s -> p s e"))
-
-        woven1 = [keep.tile([P, HALF, PACK], BF16, name="woven1_%d" % h, tag="woven1_%d" % h, align_bytes=64) for h in range(2)]
-        picked1 = [keep.tile([P, 2, HALF], BF16, name="picked1_%d" % h) for h in range(2)]
+                nc.scalar.activation(picked0[h][:, e, :], x0[:, 2 + e, :].indirect(offs_half[h]), COPY)
         for h in range(2):
-            nc.vector.tensor_copy(picked1[h][:, 0, :], plane0[:].indirect(offs_half[h]))
-        codes0 = keep.tile([P, S], U32, name="codes0", tag="plane0", align_bytes=ALIGN)
+            nc.scalar.copy(woven0[:, h * HALF : (h + 1) * HALF, 2:4], picked0[h][:].rearrange("p e s -> p s e"))
+        codes0 = keep.tile([P, S], U32, name="codes0", align_bytes=ALIGN)
         scale0 = keep.tile([P, S], U8, name="scale0", align_bytes=64)
         nc.vector.quantize_mx(out=codes0[:].bitcast(FP8X4), scales=scale0[:], in_=woven0[:].rearrange("p s j -> p (s j)"))
-        for h in (1, 0):
-            nc.vector.tensor_copy(picked1[h][:, 1, :], plane1[:].indirect(offs_half[h]))
-        nc.scalar.copy(woven1[1][:, :, 0:2], picked1[1][:].rearrange("p e s -> p s e"))
-        nc.vector.tensor_copy(woven1[0][:, :, 0:2], picked1[0][:].rearrange("p e s -> p s e"))
 
         banks = [psum.tile([M, GROUP], F32, name="bank_%d" % g) for g in range(4)]
         for g, bank in enumerate(banks):
@@ -116,32 +93,32 @@ def tile_picked_grand_none_e_kernel(tc, xT, w1_words, w1_scales, gate, offs, cen
                 stop=False,
             )
 
+        woven_first = keep.tile([P, HALF, PACK], BF16, name="woven_first", align_bytes=64)
+        woven_last = [keep.tile([P, GROUP, PACK], BF16, name="woven_last_%d" % g, tag="woven_last_%d" % g, align_bytes=64) for g in range(2)]
+        woven1 = [woven_first[:, :GROUP, :], woven_first[:, GROUP:, :], woven_last[0][:], woven_last[1][:]]
+        early = [keep.tile([P, 2, GROUP], F32, name="early_%d" % g) for g in range(2)]
+        for j in range(2):
+            nc.vector.tensor_copy(woven_first[:, :, j], x1_pair[:, j, :].indirect(offs_half[0]))
         for g in range(2):
-            third = keep.tile([P, GROUP], BF16, name="third_%d" % g)
-            nc.vector.tensor_copy(third[:], plane2[:].indirect(offs_group[2 + g]))
-            nc.scalar.copy(woven1[1][:, g * GROUP : (g + 1) * GROUP, 2], third[:])
+            for j in range(2):
+                nc.scalar.activation(early[g][:, j, :], x1_pair[:, j, :].indirect(offs_group[2 + g]), COPY)
+        for g in range(2):
+            nc.scalar.copy(woven1[2 + g][:, :, 0:2], early[g][:].rearrange("p e s -> p s e"))
         late = [keep.tile([P, 2, GROUP], BF16, name="late_%d" % g) for g in range(2)]
-        for g in range(2):
-            nc.vector.tensor_copy(late[g][:, 0, :], plane2[:].indirect(offs_group[g]))
-        plane3_bf = keep.tile([P, T], BF16, name="plane3_bf", tag="plane3_bf")
-        for a, b in VECTOR_CASTS:
-            nc.vector.tensor_copy(plane3_bf[:, a:b], plane3[:, a:b])
-        for a, b in SCALAR_CASTS:
-            nc.scalar.copy(plane3_bf[:, a:b], plane3[:, a:b])
-        for g in range(2):
-            nc.vector.tensor_copy(late[g][:, 1, :], plane3[:].indirect(offs_group[g]))
-        for g in range(2):
-            nc.vector.tensor_copy(woven1[0][:, g * GROUP : (g + 1) * GROUP, 2:4], late[g][:].rearrange("p e s -> p s e"))
-        nc.scalar.activation(woven1[1][:, :, 3], plane3_bf[:].indirect(offs_half[1]), COPY)
-        y = keep.tile([M, S], F32, name="y", tag="plane3_bf")
+        for e, plane in enumerate((plane2, plane3)):
+            nc.vector.tensor_copy(woven_first[:, :, 2 + e], plane[:].indirect(offs_half[0]))
+            for g in range(2):
+                nc.scalar.activation(late[g][:, e, :], plane[:].indirect(offs_group[2 + g]), COPY)
+        nc.scalar.copy(woven1[2][:, :, 2:4], late[0][:].rearrange("p e s -> p s e"))
+        nc.vector.tensor_copy(woven1[3][:, :, 2:4], late[1][:].rearrange("p e s -> p s e"))
+        y = keep.tile([M, S], F32, name="y")
         for g, bank in enumerate(banks):
-            h, lo = divmod(g * GROUP, HALF)
             codes1 = keep.tile([P, GROUP], U32, name="codes1_%d" % g, align_bytes=64)
             scale1 = keep.tile([P, GROUP], U8, name="scale1_%d" % g, align_bytes=64)
             nc.vector.quantize_mx(
                 out=codes1[:].bitcast(FP8X4),
                 scales=scale1[:],
-                in_=woven1[h][:, lo : lo + GROUP, :].rearrange("p s j -> p (s j)"),
+                in_=woven1[g].rearrange("p s j -> p (s j)"),
             )
             nc.tensor.matmul_mx(
                 out=bank[:],
@@ -152,28 +129,31 @@ def tile_picked_grand_none_e_kernel(tc, xT, w1_words, w1_scales, gate, offs, cen
                 start=False,
                 stop=True,
             )
-        centre_w = keep.tile([P, V], F32, name="centre_w", tag="woven1_1", align_bytes=64)
+        centre_w = keep.tile([P, V], F32, name="centre_w", tag="woven_last_1", align_bytes=64)
         nc.vector.scalar_tensor_tensor(centre_w[:], gates[:, 0, :], 1.0, gates[:, 1, :], ALU.subtract, ALU.add)
         for g, bank in enumerate(banks):
             nc.scalar.copy(y[:, g * GROUP : (g + 1) * GROUP], bank[:])
 
+        H = V // 2
+        lo, hi = slice(0, H), slice(H, V)
+        y_cen = keep.tile([M, V], F32, name="y_cen")
+        y_pos2 = keep.tile([M, H], F32, name="y_pos2")
+        nc.scalar.activation(y_cen[:], y[:].indirect(cen_sb[:]), COPY)
+        nc.scalar.activation(y_pos2[:], y[:].indirect(pos2_sb[:, H // 16 :]), COPY)
         t1 = keep.tile([M, V], F32, name="t1")
-        t2 = keep.tile([M, V], F32, name="t2")
-        nc.vector.tensor_tensor(t1[:], y[:].indirect(pos1_sb[:]), gates[:, 0, :], ALU.mult)
-        nc.vector.tensor_tensor(t2[:], y[:].indirect(pos2_sb[:]), gates[:, 1, :], ALU.mult)
-        t0 = [keep.tile([M, b - a], F32, name="t0_%d" % a) for a, b in PARTS]
-        pull = keep.tile([M, V], F32, name="pull")
+        t2_lo = keep.tile([M, H], F32, name="t2_lo")
+        t2_hi = keep.tile([M, H], F32, name="t2_hi")
+        t0 = keep.tile([M, V], F32, name="t0")
+        part_lo = keep.tile([M, H], F32, name="part_lo")
+        part_hi = keep.tile([M, H], F32, name="part_hi")
         res = keep.tile([M, V], F32, name="res", align_bytes=ALIGN)
-
-        def centre_term(i):
-            a, b = PARTS[i]
-            nc.vector.tensor_tensor(t0[i][:], y[:].indirect(cen_sb[:, a // 16 : b // 16]), centre_w[:, a:b], ALU.mult)
-
-        centre_term(0)
-        nc.vector.tensor_tensor(pull[:], t1[:], t2[:], ALU.add)
-        centre_term(1)
-        centre_term(2)
-        for i, (a, b) in enumerate(PARTS):
-            nc.vector.tensor_tensor(res[:, a:b], pull[:, a:b], t0[i][:], ALU.subtract)
-        for a, b in STORES:
-            nc.sync.dma_start(out=out[:, a:b], in_=res[:, a:b])
+        nc.vector.tensor_tensor(t1[:], y[:].indirect(pos1_sb[:]), gates[:, 0, :], ALU.mult)
+        nc.vector.tensor_tensor(t2_lo[:], y[:].indirect(pos2_sb[:, : H // 16]), gates[:, 1, lo], ALU.mult)
+        nc.vector.tensor_tensor(t0[:], y_cen[:], centre_w[:], ALU.mult)
+        nc.vector.tensor_tensor(part_lo[:], t1[:, lo], t2_lo[:], ALU.add)
+        nc.vector.tensor_tensor(t2_hi[:], y_pos2[:], gates[:, 1, hi], ALU.mult)
+        nc.vector.tensor_tensor(part_hi[:], t1[:, hi], t0[:, hi], ALU.subtract)
+        nc.vector.tensor_tensor(res[:, lo], part_lo[:], t0[:, lo], ALU.subtract)
+        nc.vector.tensor_tensor(res[:, hi], part_hi[:], t2_hi[:], ALU.add)
+        for cols in (lo, hi):
+            nc.sync.dma_start(out=out[:, cols], in_=res[:, cols])

@@ -33,7 +33,7 @@ def tile_picked_grand_none_e_kernel(tc, xT, w1_words, w1_scales, gate, offs, cen
         x0 = keep.tile([P, PACK, T], F32, name="x0", align_bytes=ALIGN)
         x1_pair = keep.tile([P, 2, T], F32, name="x1_pair", align_bytes=ALIGN)
         plane2 = keep.tile([P, T], F32, name="plane2", align_bytes=ALIGN)
-        plane3 = keep.tile([P, T], F32, name="plane3", align_bytes=ALIGN)
+        plane3 = keep.tile([P, T], F32, name="plane3", tag="plane3", align_bytes=ALIGN)
         offs_sb = keep.tile([P, S // 16], U16, name="offs_sb", align_bytes=ALIGN)
         cen_sb = keep.tile([P, V // 16], U16, name="cen_sb", align_bytes=ALIGN)
         pos1_sb = keep.tile([P, V // 16], U16, name="pos1_sb", align_bytes=ALIGN)
@@ -48,8 +48,8 @@ def tile_picked_grand_none_e_kernel(tc, xT, w1_words, w1_scales, gate, offs, cen
         nc.vector.memset(warm[:, 0:1], 0.0)
         nc.scalar.activation(warm[:, 1:2], warm[:, 0:1], COPY)
 
-        nc.sync.dma_start(offs_sb[:], offs)
         nc.sync.dma_start(out=x0[:], in_=by_pass[0])
+        nc.sync.dma_start(offs_sb[:], offs)
         for q in range(4):
             nc.sync.dma_start(
                 out=w_scale[32 * q : 32 * q + 4, :, :].bitcast(I32),
@@ -112,11 +112,12 @@ def tile_picked_grand_none_e_kernel(tc, xT, w1_words, w1_scales, gate, offs, cen
         nc.scalar.copy(woven1[2][:, :, 2:4], late[0][:].rearrange("p e s -> p s e"))
         nc.vector.tensor_copy(woven1[3][:, :, 2:4], late[1][:].rearrange("p e s -> p s e"))
         y = keep.tile([M, S], F32, name="y")
+        codes1 = keep.tile([P, S], U32, name="codes1", tag="plane3", align_bytes=ALIGN)
         for g, bank in enumerate(banks):
-            codes1 = keep.tile([P, GROUP], U32, name="codes1_%d" % g, align_bytes=64)
+            cols = slice(g * GROUP, (g + 1) * GROUP)
             scale1 = keep.tile([P, GROUP], U8, name="scale1_%d" % g, align_bytes=64)
             nc.vector.quantize_mx(
-                out=codes1[:].bitcast(FP8X4),
+                out=codes1[:, cols].bitcast(FP8X4),
                 scales=scale1[:],
                 in_=woven1[g].rearrange("p s j -> p (s j)"),
             )
@@ -124,7 +125,7 @@ def tile_picked_grand_none_e_kernel(tc, xT, w1_words, w1_scales, gate, offs, cen
                 out=bank[:],
                 lhsT=w_codes[:, 1, :].bitcast(FP8X4),
                 lhsT_scale=w_scale[:, 1, :],
-                rhs=codes1[:].bitcast(FP8X4),
+                rhs=codes1[:, cols].bitcast(FP8X4),
                 rhs_scale=scale1[:],
                 start=False,
                 stop=True,

@@ -59,10 +59,10 @@ def tile_picked_grand_none_e_kernel(tc, xT, w1_words, w1_scales, gate, offs, cen
         nc.sync.dma_start(out=plane2[:], in_=by_pass[1][:, 2, :])
         nc.sync.dma_start(out=plane3[:], in_=by_pass[1][:, 3, :])
         nc.sync.dma_start(out=w_codes[:].bitcast(I32), in_=w1_words.rearrange("z p c r -> p z (c r)").bitcast(I32))
-        nc.sync.dma_start(out=gates[:], in_=gate.rearrange("d p v -> p d v"))
         nc.sync.dma_start(pos1_sb[:], pos1)
         nc.sync.dma_start(cen_sb[:], cen)
         nc.sync.dma_start(pos2_sb[:], pos2)
+        nc.sync.dma_start(out=gates[:], in_=gate.rearrange("d p v -> p d v"))
 
         offs_half = [offs_sb[:, h * HALF // 16 : (h + 1) * HALF // 16] for h in range(2)]
         offs_group = [offs_sb[:, g * GROUP // 16 : (g + 1) * GROUP // 16] for g in range(4)]

@@ -48,17 +48,22 @@ def tile_picked_grand_none_e_kernel(tc, xT, w1_words, w1_scales, gate, offs, cen
         nc.vector.memset(warm[:, 0:1], 0.0)
         nc.scalar.activation(warm[:, 1:2], warm[:, 0:1], COPY)
 
-        nc.sync.dma_start(out=x0[:], in_=by_pass[0])
-        nc.sync.dma_start(offs_sb[:], offs)
-        for q in range(4):
+        def load_scale_rows(q):
             nc.sync.dma_start(
                 out=w_scale[32 * q : 32 * q + 4, :, :].bitcast(I32),
                 in_=w1_scales[:, 4 * q : 4 * q + 4, :].rearrange("z r c -> r z c").bitcast(I32),
             )
+
+        nc.sync.dma_start(out=x0[:], in_=by_pass[0])
+        nc.sync.dma_start(offs_sb[:], offs)
+        for q in range(2):
+            load_scale_rows(q)
         nc.sync.dma_start(out=x1_pair[:], in_=by_pass[1][:, 0:2, :])
         nc.sync.dma_start(out=plane2[:], in_=by_pass[1][:, 2, :])
         nc.sync.dma_start(out=plane3[:], in_=by_pass[1][:, 3, :])
         nc.sync.dma_start(out=w_codes[:].bitcast(I32), in_=w1_words.rearrange("z p c r -> p z (c r)").bitcast(I32))
+        for q in range(2, 4):
+            load_scale_rows(q)
         nc.sync.dma_start(pos1_sb[:], pos1)
         nc.sync.dma_start(cen_sb[:], cen)
         nc.sync.dma_start(pos2_sb[:], pos2)
@@ -153,8 +158,11 @@ def tile_picked_grand_none_e_kernel(tc, xT, w1_words, w1_scales, gate, offs, cen
         nc.vector.tensor_tensor(t0[:], y_cen[:], centre_w[:], ALU.mult)
         nc.vector.tensor_tensor(part_lo[:], t1[:, lo], t2_lo[:], ALU.add)
         nc.vector.tensor_tensor(t2_hi[:], y_pos2[:], gates[:, 1, hi], ALU.mult)
-        nc.vector.tensor_tensor(part_hi[:], t1[:, hi], t0[:, hi], ALU.subtract)
+        Q = H // 2
+        for a in (0, Q):
+            nc.vector.tensor_tensor(part_hi[:, a : a + Q], t1[:, H + a : H + a + Q], t0[:, H + a : H + a + Q], ALU.subtract)
         nc.vector.tensor_tensor(res[:, lo], part_lo[:], t0[:, lo], ALU.subtract)
-        nc.vector.tensor_tensor(res[:, hi], part_hi[:], t2_hi[:], ALU.add)
+        for a in (0, Q):
+            nc.vector.tensor_tensor(res[:, H + a : H + a + Q], part_hi[:, a : a + Q], t2_hi[:, a : a + Q], ALU.add)
         for cols in (lo, hi):
             nc.sync.dma_start(out=out[:, cols], in_=res[:, cols])

@@ -56,11 +56,11 @@ def tile_picked_grand_none_e_kernel(tc, xT, w1_words, w1_scales, gate, offs, cen
 
         nc.sync.dma_start(out=x0[:], in_=by_pass[0])
         nc.sync.dma_start(offs_sb[:], offs)
-        for q in range(2):
-            load_scale_rows(q)
         nc.sync.dma_start(out=x1_pair[:], in_=by_pass[1][:, 0:2, :])
         nc.sync.dma_start(out=plane2[:], in_=by_pass[1][:, 2, :])
         nc.sync.dma_start(out=plane3[:], in_=by_pass[1][:, 3, :])
+        for q in range(2):
+            load_scale_rows(q)
         nc.sync.dma_start(out=w_codes[:].bitcast(I32), in_=w1_words.rearrange("z p c r -> p z (c r)").bitcast(I32))
         for q in range(2, 4):
             load_scale_rows(q)

@@ -114,8 +114,8 @@ def tile_picked_grand_none_e_kernel(tc, xT, w1_words, w1_scales, gate, offs, cen
             nc.vector.tensor_copy(woven_first[:, :, 2 + e], plane[:].indirect(offs_half[0]))
             for g in range(2):
                 nc.scalar.activation(late[g][:, e, :], plane[:].indirect(offs_group[2 + g]), COPY)
-        nc.scalar.copy(woven1[2][:, :, 2:4], late[0][:].rearrange("p e s -> p s e"))
-        nc.vector.tensor_copy(woven1[3][:, :, 2:4], late[1][:].rearrange("p e s -> p s e"))
+            nc.scalar.copy(woven1[2][:, :, 2 + e], late[0][:, e, :])
+            nc.vector.tensor_copy(woven1[3][:, :, 2 + e], late[1][:, e, :])
         y = keep.tile([M, S], F32, name="y")
         codes1 = keep.tile([P, S], U32, name="codes1", tag="plane3", align_bytes=ALIGN)
         for g, bank in enumerate(banks):

@@ -135,7 +135,7 @@ def tile_picked_grand_none_e_kernel(tc, xT, w1_words, w1_scales, gate, offs, cen
                 start=False,
                 stop=True,
             )
-        centre_w = keep.tile([P, V], F32, name="centre_w", tag="woven_last_1", align_bytes=64)
+        centre_w = keep.tile([P, V], F32, name="centre_w")
         nc.vector.scalar_tensor_tensor(centre_w[:], gates[:, 0, :], 1.0, gates[:, 1, :], ALU.subtract, ALU.add)
         for g, bank in enumerate(banks):
             nc.scalar.copy(y[:, g * GROUP : (g + 1) * GROUP], bank[:])

from contextlib import ExitStack

import concourse.mybir as mybir

K, T, S, V, M = 1024, 2048, 512, 256, 128
FLOPS = 2 * K * M * S

F32 = mybir.dt.float32
BF16 = mybir.dt.bfloat16
I32 = mybir.dt.int32
U32 = mybir.dt.uint32
U16 = mybir.dt.uint16
U8 = mybir.dt.uint8
FP8X4 = mybir.dt.float8_e4m3fn_x4
ALU = mybir.AluOpType
COPY = mybir.ActivationFunctionType.Copy

P = 128
PACK = 4
PASSES = K // (P * PACK)
HALF = S // 2
GROUP = 128
ALIGN = 256


def tile_picked_grand_none_e_kernel(tc, xT, w1_words, w1_scales, gate, offs, cen, pos1, pos2, out):
    nc = tc.nc
    with ExitStack() as ctx:
        keep = ctx.enter_context(tc.tile_pool(name="keep", bufs=1))
        psum = ctx.enter_context(tc.psum_pool(name="psum", bufs=1))

        by_pass = xT.rearrange("(z p j) t -> z p j t", p=P, j=PACK)
        x0 = keep.tile([P, PACK, T], F32, name="x0", align_bytes=ALIGN)
        x1_pair = keep.tile([P, 2, T], F32, name="x1_pair", align_bytes=ALIGN)
        plane2 = keep.tile([P, T], F32, name="plane2", align_bytes=ALIGN)
        plane3 = keep.tile([P, T], F32, name="plane3", tag="plane3", align_bytes=ALIGN)
        offs_sb = keep.tile([P, S // 16], U16, name="offs_sb", align_bytes=ALIGN)
        cen_sb = keep.tile([P, V // 16], U16, name="cen_sb", align_bytes=ALIGN)
        pos1_sb = keep.tile([P, V // 16], U16, name="pos1_sb", align_bytes=ALIGN)
        pos2_sb = keep.tile([P, V // 16], U16, name="pos2_sb", align_bytes=ALIGN)
        w_codes = keep.tile([P, PASSES, M], U32, name="w_codes", align_bytes=ALIGN)
        w_scale = keep.tile([P, PASSES, M], U8, name="w_scale", align_bytes=ALIGN)
        gates = keep.tile([P, 2, V], F32, name="gates", align_bytes=ALIGN)

        nc.vector.memset(w_scale[:].bitcast(I32), 0)

        warm = keep.tile([P, 2], F32, name="warm")
        nc.vector.memset(warm[:, 0:1], 0.0)
        nc.scalar.activation(warm[:, 1:2], warm[:, 0:1], COPY)

        def load_scale_rows(q):
            nc.sync.dma_start(
                out=w_scale[32 * q : 32 * q + 4, :, :].bitcast(I32),
                in_=w1_scales[:, 4 * q : 4 * q + 4, :].rearrange("z r c -> r z c").bitcast(I32),
            )

        nc.sync.dma_start(out=x0[:], in_=by_pass[0])
        nc.sync.dma_start(offs_sb[:], offs)
        nc.sync.dma_start(out=x1_pair[:], in_=by_pass[1][:, 0:2, :])
        nc.sync.dma_start(out=plane2[:], in_=by_pass[1][:, 2, :])
        nc.sync.dma_start(out=plane3[:], in_=by_pass[1][:, 3, :])
        for q in range(2):
            load_scale_rows(q)
        nc.sync.dma_start(out=w_codes[:].bitcast(I32), in_=w1_words.rearrange("z p c r -> p z (c r)").bitcast(I32))
        for q in range(2, 4):
            load_scale_rows(q)
        nc.sync.dma_start(pos1_sb[:], pos1)
        nc.sync.dma_start(cen_sb[:], cen)
        nc.sync.dma_start(pos2_sb[:], pos2)
        nc.sync.dma_start(out=gates[:], in_=gate.rearrange("d p v -> p d v"))

        offs_half = [offs_sb[:, h * HALF // 16 : (h + 1) * HALF // 16] for h in range(2)]
        offs_group = [offs_sb[:, g * GROUP // 16 : (g + 1) * GROUP // 16] for g in range(4)]

        woven0 = keep.tile([P, S, PACK], BF16, name="woven0", align_bytes=64)
        picked0 = [keep.tile([P, 2, HALF], F32, name="picked0_%d" % h) for h in range(2)]
        for j in range(2):
            nc.vector.tensor_copy(woven0[:, :, j], x0[:, j, :].indirect(offs_sb[:]))
        for h in range(2):
            for e in range(2):
                nc.scalar.activation(picked0[h][:, e, :], x0[:, 2 + e, :].indirect(offs_half[h]), COPY)
        for h in range(2):
            nc.scalar.copy(woven0[:, h * HALF : (h + 1) * HALF, 2:4], picked0[h][:].rearrange("p e s -> p s e"))
        codes0 = keep.tile([P, S], U32, name="codes0", align_bytes=ALIGN)
        scale0 = keep.tile([P, S], U8, name="scale0", align_bytes=64)
        nc.vector.quantize_mx(out=codes0[:].bitcast(FP8X4), scales=scale0[:], in_=woven0[:].rearrange("p s j -> p (s j)"))

        banks = [psum.tile([M, GROUP], F32, name="bank_%d" % g) for g in range(4)]
        for g, bank in enumerate(banks):
            cols = slice(g * GROUP, (g + 1) * GROUP)
            nc.tensor.matmul_mx(
                out=bank[:],
                lhsT=w_codes[:, 0, :].bitcast(FP8X4),
                lhsT_scale=w_scale[:, 0, :],
                rhs=codes0[:, cols].bitcast(FP8X4),
                rhs_scale=scale0[:, cols],
                start=True,
                stop=False,
            )

        woven_first = keep.tile([P, HALF, PACK], BF16, name="woven_first", align_bytes=64)
        woven_last = [keep.tile([P, GROUP, PACK], BF16, name="woven_last_%d" % g, tag="woven_last_%d" % g, align_bytes=64) for g in range(2)]
        woven1 = [woven_first[:, :GROUP, :], woven_first[:, GROUP:, :], woven_last[0][:], woven_last[1][:]]
        early = [keep.tile([P, 2, GROUP], F32, name="early_%d" % g) for g in range(2)]
        for j in range(2):
            nc.vector.tensor_copy(woven_first[:, :, j], x1_pair[:, j, :].indirect(offs_half[0]))
        for g in range(2):
            for j in range(2):
                nc.scalar.activation(early[g][:, j, :], x1_pair[:, j, :].indirect(offs_group[2 + g]), COPY)
        for g in range(2):
            nc.scalar.copy(woven1[2 + g][:, :, 0:2], early[g][:].rearrange("p e s -> p s e"))
        late = [keep.tile([P, 2, GROUP], BF16, name="late_%d" % g) for g in range(2)]
        for e, plane in enumerate((plane2, plane3)):
            nc.vector.tensor_copy(woven_first[:, :, 2 + e], plane[:].indirect(offs_half[0]))
            for g in range(2):
                nc.scalar.activation(late[g][:, e, :], plane[:].indirect(offs_group[2 + g]), COPY)
            nc.scalar.copy(woven1[2][:, :, 2 + e], late[0][:, e, :])
            nc.vector.tensor_copy(woven1[3][:, :, 2 + e], late[1][:, e, :])
        y = keep.tile([M, S], F32, name="y")
        codes1 = keep.tile([P, S], U32, name="codes1", tag="plane3", align_bytes=ALIGN)
        for g, bank in enumerate(banks):
            cols = slice(g * GROUP, (g + 1) * GROUP)
            scale1 = keep.tile([P, GROUP], U8, name="scale1_%d" % g, align_bytes=64)
            nc.vector.quantize_mx(
                out=codes1[:, cols].bitcast(FP8X4),
                scales=scale1[:],
                in_=woven1[g].rearrange("p s j -> p (s j)"),
            )
            nc.tensor.matmul_mx(
                out=bank[:],
                lhsT=w_codes[:, 1, :].bitcast(FP8X4),
                lhsT_scale=w_scale[:, 1, :],
                rhs=codes1[:, cols].bitcast(FP8X4),
                rhs_scale=scale1[:],
                start=False,
                stop=True,
            )
        centre_w = keep.tile([P, V], F32, name="centre_w")
        nc.vector.scalar_tensor_tensor(centre_w[:], gates[:, 0, :], 1.0, gates[:, 1, :], ALU.subtract, ALU.add)
        for g, bank in enumerate(banks):
            nc.scalar.copy(y[:, g * GROUP : (g + 1) * GROUP], bank[:])

        H = V // 2
        lo, hi = slice(0, H), slice(H, V)
        y_cen = keep.tile([M, V], F32, name="y_cen")
        y_pos2 = keep.tile([M, H], F32, name="y_pos2")
        nc.scalar.activation(y_cen[:], y[:].indirect(cen_sb[:]), COPY)
        nc.scalar.activation(y_pos2[:], y[:].indirect(pos2_sb[:, H // 16 :]), COPY)
        t1 = keep.tile([M, V], F32, name="t1")
        t2_lo = keep.tile([M, H], F32, name="t2_lo")
        t2_hi = keep.tile([M, H], F32, name="t2_hi")
        t0 = keep.tile([M, V], F32, name="t0")
        part_lo = keep.tile([M, H], F32, name="part_lo")
        part_hi = keep.tile([M, H], F32, name="part_hi")
        res = keep.tile([M, V], F32, name="res", align_bytes=ALIGN)
        nc.vector.tensor_tensor(t1[:], y[:].indirect(pos1_sb[:]), gates[:, 0, :], ALU.mult)
        nc.vector.tensor_tensor(t2_lo[:], y[:].indirect(pos2_sb[:, : H // 16]), gates[:, 1, lo], ALU.mult)
        nc.vector.tensor_tensor(t0[:], y_cen[:], centre_w[:], ALU.mult)
        nc.vector.tensor_tensor(part_lo[:], t1[:, lo], t2_lo[:], ALU.add)
        nc.vector.tensor_tensor(t2_hi[:], y_pos2[:], gates[:, 1, hi], ALU.mult)
        Q = H // 2
        for a in (0, Q):
            nc.vector.tensor_tensor(part_hi[:, a : a + Q], t1[:, H + a : H + a + Q], t0[:, H + a : H + a + Q], ALU.subtract)
        nc.vector.tensor_tensor(res[:, lo], part_lo[:], t0[:, lo], ALU.subtract)
        for a in (0, Q):
            nc.vector.tensor_tensor(res[:, H + a : H + a + Q], part_hi[:, a : a + Q], t2_hi[:, a : a + Q], ALU.add)
        for cols in (lo, hi):
            nc.sync.dma_start(out=out[:, cols], in_=res[:, cols])
